import numpy as np
import ml_dtypes


def mxq(x, axis, fmt="e4m3"):
    dtype, down = {"e4m3": (ml_dtypes.float8_e4m3fn, 7), "e5m2": (ml_dtypes.float8_e5m2, 14)}[fmt]
    v = np.moveaxis(np.asarray(x, np.float32).astype(ml_dtypes.bfloat16).astype(np.float64), axis, -1)
    blocks = v.reshape(v.shape[:-1] + (-1, 32))
    amax = np.abs(blocks).max(-1, keepdims=True)
    byte = np.maximum(np.where(amax > 0, np.frexp(amax)[1] - 1 + 127, 0) - down, 1)
    scale = np.exp2(byte - 127.0)
    codes = (blocks / scale).astype(np.float32).astype(dtype).astype(np.float64)
    return np.moveaxis((codes * scale).reshape(v.shape), -1, axis)


WIDE = False


def mx_kscale(k):
    if not WIDE:
        return np.ones(k)
    levels = np.array([24, -24, 12, -12, 0])
    if k % 512:
        return np.exp2(np.random.permutation(np.resize(levels, k // 32))).repeat(32)
    a = np.empty((k // 512, 16))
    for p in range(k // 512):
        a[p, :8] = np.random.permutation(np.resize(levels, 8))
        for g in range(8):
            far = levels[np.abs(levels - a[p, g]) >= 10]
            a[p, g + 8] = far[np.random.randint(len(far))]
    return np.exp2(a.ravel()).repeat(32)


def f64(x):
    return np.asarray(x).astype(np.float64)


E2M1 = np.array([0.0, 0.5, 1.0, 1.5, 2.0, 3.0, 4.0, 6.0, -0.0, -0.5, -1.0, -1.5, -2.0, -3.0, -4.0, -6.0])


def pack_weight(w, fmt):
    k, n = w.shape
    w = f64(np.asarray(w, np.float32).astype(ml_dtypes.bfloat16)).reshape(k // 32, 32, n)
    amax = np.abs(w).max(1)
    if fmt == "e4m3":
        byte = np.frexp(amax)[1] - 1 + 127 - 7
    else:
        mant, ex = np.frexp(amax / 6.0)
        byte = np.where(mant > 0.5, ex, ex - 1) + 127
    byte = np.clip(np.where(amax > 0, byte, 1), 1, 254)
    scaled = (w * np.exp2(127.0 - byte)[:, None, :]).reshape(k, n).astype(np.float32)
    by_word = np.ascontiguousarray(scaled.reshape(k // 512, 128, 4, n).transpose(0, 1, 3, 2))
    if fmt == "e4m3":
        words = by_word.astype(ml_dtypes.float8_e4m3fn).view(np.uint8)
    else:
        c = by_word.astype(ml_dtypes.float4_e2m1fn).view(np.uint8) & 0xF
        words = (c[..., 0::2] | (c[..., 1::2] << 4)).reshape(k // 512, 128, 2 * n)
    return np.ascontiguousarray(words), np.ascontiguousarray(byte.astype(np.uint8).reshape(k // 512, 16, n))


def unpack_weight(words, scales, fmt):
    g, _, n = scales.shape
    words = np.ascontiguousarray(words).reshape(g, 128, n, -1)
    if fmt == "e4m3":
        vals = words.view(ml_dtypes.float8_e4m3fn).astype(np.float64)
    else:
        nib = np.empty((g, 128, n, 4), np.uint8)
        nib[..., 0::2] = words & 0xF
        nib[..., 1::2] = words >> 4
        vals = E2M1[nib]
    vals = vals * np.repeat(np.exp2(scales.astype(np.float64) - 127.0), 8, axis=1)[..., None]
    return vals.transpose(0, 1, 3, 2).reshape(g * 512, n)


K, R, N, T = 1024, 512, 512, 1024


def setup_inputs():
    n = np.random.standard_normal
    s = mx_kscale(K)[:, None]
    u = mx_kscale(R)[:, None]
    p_wb = pack_weight(0.7 * n((K, N)) / np.sqrt(K) / s, "e2m1")
    p_dn = pack_weight(n((K, R)) / np.sqrt(K) / s * u.T, "e4m3")
    p_upw = pack_weight(n((R, N)) / np.sqrt(R) / u, "e4m3")
    return {
        "x": (n((K, T)) * s).astype(np.float32),
        "wb_words": p_wb[0],
        "wb_scales": p_wb[1],
        "dn_words": p_dn[0],
        "dn_scales": p_dn[1],
        "upw_words": p_upw[0],
        "upw_scales": p_upw[1],
        "x0": (n((N, T))).astype(np.float32),
        "b": (0.3 * n(N)).astype(np.float32),
        "xr": (n((N, T))).astype(np.float32),
    }


def reference(x, wb_words, wb_scales, dn_words, dn_scales, upw_words, upw_scales, x0, b, xr):
    x_ = mxq(f64(x), 0, "e4m3")
    wb_ = unpack_weight(wb_words, wb_scales, "e2m1")
    dn_ = unpack_weight(dn_words, dn_scales, "e4m3")
    upw_ = unpack_weight(upw_words, upw_scales, "e4m3")
    hs = dn_.T @ x_
    h_ = mxq(hs, 0, "e4m3")
    y = wb_.T @ x_ + upw_.T @ h_
    return f64(x0) * (y + f64(b)[:, None]) + f64(xr)

@@ -1,0 +1,259 @@
+from contextlib import ExitStack
+
+import concourse.mybir as mybir
+from concourse.masks import make_identity
+
+K, R, N, T = 1024, 512, 512, 1024
+FLOPS = 2 * T * (K * R + K * N + R * N)
+
+F32 = mybir.dt.float32
+BF16 = mybir.dt.bfloat16
+I32 = mybir.dt.int32
+U8 = mybir.dt.uint8
+FP8X4 = mybir.dt.float8_e4m3fn_x4
+FP4X4 = mybir.dt.float4_e2m1fn_x4
+ADD = mybir.AluOpType.add
+MULT = mybir.AluOpType.mult
+
+P = 128
+PACK = 4
+PASSES = K // (P * PACK)
+HALF = 512
+CH = 128
+NCH = HALF // CH
+NT = N // P
+
+
+def tile_mix_cross_none_kernel(tc, x, wb_words, wb_scales, dn_words, dn_scales, upw_words, upw_scales, x0, b, xr, out):
+    nc = tc.nc
+    with ExitStack() as ctx:
+        sb = ctx.enter_context(tc.tile_pool(name="sb", bufs=1))
+        ps = ctx.enter_context(tc.psum_pool(name="ps", bufs=1))
+        ctx.enter_context(tc.manual_schedule())
+
+        def tl(name, shape, dtype):
+            return sb.tile(shape, dtype, name=name, align_bytes=64)
+
+        dn_raw = tl("dn_raw", [P, PASSES, R], I32)
+        dn_sraw = tl("dn_sraw", [P, PASSES, R], U8)
+        dn_w = [tl("dn_w%d" % a, [P, R], I32) for a in range(PASSES)]
+        dn_s = [tl("dn_s%d" % a, [P, R], U8) for a in range(PASSES)]
+        wb_w = tl("wb_w", [P, PASSES, 2 * N], U8)
+        wb_s = tl("wb_s", [P, PASSES, N], U8)
+        up_w = tl("up_w", [P, N], I32)
+        up_s = tl("up_s", [P, 1, N], U8)
+        b_rows = tl("b_rows", [P, P], F32)
+        b_col = tl("b_col", [P, NT], F32)
+        ident = tl("ident", [P, P], F32)
+        x_first = tl("x_first", [P, PACK, T], F32)
+        x_second = [tl("x_second%d" % h, [P, PACK, HALF], F32) for h in range(2)]
+        xq = {(a, h): tl("xq%d%d" % (a, h), [P, HALF], I32) for a in range(2) for h in range(2)}
+        xs = {(a, h): tl("xs%d%d" % (a, h), [P, HALF], U8) for a in range(2) for h in range(2)}
+        hq = [tl("hq%d" % h, [P, HALF], I32) for h in range(2)]
+        hs = [tl("hs%d" % h, [P, HALF], U8) for h in range(2)]
+        x0_sb = [tl("x0_sb%d" % c, [P, T], F32) for c in range(NT)]
+        xr_sb = [tl("xr_sb%d" % c, [P, T], F32) for c in range(NT)]
+        res = [tl("res%d" % c, [P, T], F32) for c in range(NT)]
+        xg, hg, prod, hbank, ybank = {}, {}, {}, {}, {}
+
+        def load_scales(eng, plane, scales, quads):
+            for q in quads:
+                eng.dma_start(
+                    out=plane[32 * q : 32 * q + 4].bitcast(I32),
+                    in_=scales[:, 4 * q : 4 * q + 4, :].rearrange("a r n -> r a n").bitcast(I32),
+                )
+
+        def zero(eng, plane):
+            eng.memset(plane[:].rearrange("p a n -> p (a n)").bitcast(I32), 0)
+
+        def cast(eng, a, h, c0, c1):
+            w = (c1 - c0) * CH
+            g = tl("xg%d%d%d" % (a, h, c0), [P, w * PACK], BF16)
+            xg[a, h, c0] = g
+            if a == 0:
+                src = x_first[:, :, h * HALF + c0 * CH : h * HALF + c1 * CH]
+            else:
+                src = x_second[h][:, :, c0 * CH : c1 * CH]
+            o = g[:].rearrange("p (c i j) -> p c j i", i=4, j=PACK)
+            s = src.rearrange("p j (c i) -> p c j i", i=4)
+            if eng == "v":
+                nc.vector.tensor_copy(out=o, in_=s)
+            else:
+                nc.scalar.copy(out=o, in_=s)
+
+        def quant_x(a, h, c0, c1):
+            cols = slice(c0 * CH, c1 * CH)
+            nc.vector.quantize_mx(out=xq[a, h][:, cols].bitcast(FP8X4), scales=xs[a, h][:, cols], in_=xg[a, h, c0][:])
+
+        def h_mm(a, h, ch):
+            if a == 0:
+                hbank[h, ch] = ps.tile([P, PACK, CH], F32, name="bank_a%d" % ch)
+            cols = slice(ch * CH, (ch + 1) * CH)
+            for j in range(PACK):
+                nc.tensor.matmul_mx(
+                    out=hbank[h, ch][:, j, :],
+                    lhsT=dn_w[a][:, j * P : (j + 1) * P].bitcast(FP8X4),
+                    lhsT_scale=dn_s[a][:, j * P : (j + 1) * P],
+                    rhs=xq[a, h][:, cols].bitcast(FP8X4),
+                    rhs_scale=xs[a, h][:, cols],
+                    start=(a == 0 and j == 0),
+                    stop=(a == PASSES - 1 and j == PACK - 1),
+                )
+
+        def h_copy(h, ch):
+            g = tl("hg%d%d" % (h, ch), [P, CH * PACK], BF16)
+            hg[h, ch] = g
+            nc.scalar.copy(out=g[:].rearrange("p (t j) -> p t j", j=PACK), in_=hbank[h, ch][:].rearrange("p j t -> p t j"))
+
+        def quant_h(h, ch):
+            cols = slice(ch * CH, (ch + 1) * CH)
+            nc.vector.quantize_mx(out=hq[h][:, cols].bitcast(FP8X4), scales=hs[h][:, cols], in_=hg[h, ch][:])
+
+        def y_wb(a, h, c):
+            if a == 0:
+                ybank[h, c] = ps.tile([P, HALF], F32, name=("bank_b%d" if h == 0 else "bank_a%d") % c)
+            nc.tensor.matmul_mx(
+                out=ybank[h, c][:],
+                lhsT=wb_w[:, a, 2 * c * P : 2 * (c + 1) * P].bitcast(FP4X4),
+                lhsT_scale=wb_s[:, a, c * P : (c + 1) * P],
+                rhs=xq[a, h][:].bitcast(FP8X4),
+                rhs_scale=xs[a, h][:],
+                start=(a == 0),
+                stop=False,
+            )
+
+        def y_up(h, c):
+            nc.tensor.matmul_mx(
+                out=ybank[h, c][:],
+                lhsT=up_w[:, c * P : (c + 1) * P].bitcast(FP8X4),
+                lhsT_scale=up_s[:, 0, c * P : (c + 1) * P],
+                rhs=hq[h][:].bitcast(FP8X4),
+                rhs_scale=hs[h][:],
+                start=False,
+                stop=True,
+            )
+
+        def gate(c, h):
+            cols = slice(h * HALF, (h + 1) * HALF)
+            u = tl("prod%d%d" % (c, h), [P, HALF], F32)
+            prod[c, h] = u
+            nc.vector.scalar_tensor_tensor(out=u[:], in0=ybank[h, c][:], scalar=b_col[:, c : c + 1], in1=x0_sb[c][:, cols], op0=ADD, op1=MULT)
+
+        def resid(c, h):
+            cols = slice(h * HALF, (h + 1) * HALF)
+            nc.vector.tensor_tensor(out=res[c][:, cols], in0=prod[c, h][:], in1=xr_sb[c][:, cols], op=ADD)
+
+        def store(c):
+            nc.sync.dma_start(out=out[c * P : (c + 1) * P, :], in_=res[c][:])
+
+        zero(nc.vector, dn_sraw)
+        zero(nc.vector, wb_s)
+        zero(nc.vector, up_s)
+        nc.gpsimd.memset(b_rows[:], 0.0)
+        make_identity(nc, ident[:])
+
+        xv = x.rearrange("(a p j) t -> a p j t", p=P, j=PACK)
+        nc.sync.dma_start(out=dn_raw[:], in_=dn_words.rearrange("a p r i -> p a (r i)").bitcast(I32))
+        load_scales(nc.scalar, dn_sraw, dn_scales, range(4))
+        nc.scalar.dma_start(out=b_rows[0:NT, :], in_=b.rearrange("(c p) -> c p", p=P))
+        load_scales(nc.scalar, wb_s, wb_scales, range(1))
+        nc.sync.dma_start(out=x_first[:], in_=xv[0])
+        nc.sync.dma_start(out=wb_w[:].bitcast(I32), in_=wb_words.rearrange("a p n -> p a n").bitcast(I32))
+        load_scales(nc.scalar, wb_s, wb_scales, range(1, 4))
+        load_scales(nc.scalar, up_s, upw_scales, range(1))
+        nc.sync.dma_start(out=x_second[0][:], in_=xv[1][:, :, 0:HALF])
+        load_scales(nc.scalar, up_s, upw_scales, range(1, 2))
+        nc.sync.dma_start(out=x_second[1][:], in_=xv[1][:, :, HALF:T])
+        nc.sync.dma_start(out=up_w[:], in_=upw_words[0].rearrange("p n i -> p (n i)").bitcast(I32))
+        load_scales(nc.scalar, up_s, upw_scales, range(2, 4))
+        for c in range(NT):
+            nc.sync.dma_start(out=x0_sb[c][:], in_=x0[c * P : (c + 1) * P, :])
+            nc.sync.dma_start(out=xr_sb[c][:], in_=xr[c * P : (c + 1) * P, :])
+
+        for a in range(PASSES):
+            nc.vector.tensor_copy(
+                out=dn_w[a][:].rearrange("p (j mo mi) -> p mo j mi", j=PACK, mi=4),
+                in_=dn_raw[:, a, :].rearrange("p (mo mi j) -> p mo j mi", j=PACK, mi=4),
+            )
+        for a in range(PASSES):
+            nc.vector.tensor_copy(
+                out=dn_s[a][:].rearrange("p (j m) -> p m j", j=PACK),
+                in_=dn_sraw[:, a, :].rearrange("p (m j) -> p m j", j=PACK),
+            )
+
+        bt = ps.tile([P, HALF], F32, name="bank_b0")
+        nc.tensor.transpose(bt[:, 0:P], b_rows[:], ident[:])
+        nc.scalar.copy(out=b_col[:], in_=bt[:, 0:NT])
+
+        cast("v", 0, 0, 0, 2)
+        cast("s", 0, 0, 2, 4)
+        cast("v", 0, 1, 0, 2)
+        quant_x(0, 0, 0, 2)
+        quant_x(0, 0, 2, 4)
+        cast("s", 0, 1, 2, 4)
+        quant_x(0, 1, 0, 2)
+        for ch in range(NCH):
+            h_mm(0, 0, ch)
+        for c in range(NT):
+            y_wb(0, 0, c)
+        quant_x(0, 1, 2, 4)
+
+        def second_pass(h):
+            cast("s", 1, h, 3, 4)
+            cast("v", 1, h, 0, 1)
+            cast("v", 1, h, 1, 2)
+            quant_x(1, h, 0, 1)
+            cast("v", 1, h, 2, 3)
+            quant_x(1, h, 1, 2)
+            quant_x(1, h, 3, 4)
+            quant_x(1, h, 2, 3)
+
+        order = [0, 1, 3, 2]
+        second_pass(0)
+        for ch in order:
+            h_mm(1, 0, ch)
+            h_copy(0, ch)
+        for c in range(NT):
+            y_wb(1, 0, c)
+        for ch in order:
+            quant_h(0, ch)
+            h_mm(0, 1, ch)
+        second_pass(1)
+        for c in range(NT):
+            y_up(0, c)
+        for ch in order:
+            h_mm(1, 1, ch)
+            h_copy(1, ch)
+        gate(0, 0)
+        quant_h(1, 0)
+        resid(0, 0)
+        quant_h(1, 1)
+        quant_h(1, 3)
+        quant_h(1, 2)
+        for c in (0, 1):
+            y_wb(0, 1, c)
+            y_wb(1, 1, c)
+        for c in (0, 1):
+            y_up(1, c)
+        for c in (2, 3):
+            y_wb(0, 1, c)
+            y_wb(1, 1, c)
+            y_up(1, c)
+        gate(1, 0)
+        gate(0, 1)
+        resid(1, 0)
+        resid(0, 1)
+        store(0)
+        gate(1, 1)
+        gate(2, 0)
+        resid(1, 1)
+        store(1)
+        gate(2, 1)
+        resid(2, 0)
+        gate(3, 0)
+        resid(2, 1)
+        store(2)
+        gate(3, 1)
+        resid(3, 0)
+        resid(3, 1)
+        store(3)

@@ -35,9 +35,9 @@ def tile_mix_cross_none_kernel(tc, x, wb_words, wb_scales, dn_words, dn_scales, 
             return sb.tile(shape, dtype, name=name, align_bytes=64)
 
         dn_raw = tl("dn_raw", [P, PASSES, R], I32)
-        dn_sraw = tl("dn_sraw", [P, PASSES, R], U8)
+        dn_sraw = tl("dn_sraw", [P, R], U8)
         dn_w = [tl("dn_w%d" % a, [P, R], I32) for a in range(PASSES)]
-        dn_s = [tl("dn_s%d" % a, [P, R], U8) for a in range(PASSES)]
+        dn_s = tl("dn_s", [P, R], U8)
         wb_w = tl("wb_w", [P, PASSES, 2 * N], U8)
         wb_s = tl("wb_s", [P, PASSES, N], U8)
         up_w = tl("up_w", [P, N], I32)
@@ -45,14 +45,16 @@ def tile_mix_cross_none_kernel(tc, x, wb_words, wb_scales, dn_words, dn_scales, 
         b_rows = tl("b_rows", [P, P], F32)
         b_col = tl("b_col", [P, NT], F32)
         ident = tl("ident", [P, P], F32)
-        x_first = tl("x_first", [P, PACK, T], F32)
-        x_second = [tl("x_second%d" % h, [P, PACK, HALF], F32) for h in range(2)]
+        x_raw = {}
+        for a, h in ((0, 0), (1, 0), (0, 1)):
+            x_raw[a, h, 0] = tl("x_raw%d%d" % (a, h), [P, PACK, HALF], F32)
+        for c0 in (0, 2):
+            x_raw[1, 1, c0] = tl("x_raw11%d" % c0, [P, PACK, 2 * CH], F32)
         xq = {(a, h): tl("xq%d%d" % (a, h), [P, HALF], I32) for a in range(2) for h in range(2)}
         xs = {(a, h): tl("xs%d%d" % (a, h), [P, HALF], U8) for a in range(2) for h in range(2)}
         hq = [tl("hq%d" % h, [P, HALF], I32) for h in range(2)]
         hs = [tl("hs%d" % h, [P, HALF], U8) for h in range(2)]
-        x0_sb = [tl("x0_sb%d" % c, [P, T], F32) for c in range(NT)]
-        xr_sb = [tl("xr_sb%d" % c, [P, T], F32) for c in range(NT)]
+        x0_sb, xr_sb = {}, {}
         res = [tl("res%d" % c, [P, T], F32) for c in range(NT)]
         xg, hg, prod, hbank, ybank = {}, {}, {}, {}, {}
 
@@ -70,10 +72,8 @@ def tile_mix_cross_none_kernel(tc, x, wb_words, wb_scales, dn_words, dn_scales, 
             w = (c1 - c0) * CH
             g = tl("xg%d%d%d" % (a, h, c0), [P, w * PACK], BF16)
             xg[a, h, c0] = g
-            if a == 0:
-                src = x_first[:, :, h * HALF + c0 * CH : h * HALF + c1 * CH]
-            else:
-                src = x_second[h][:, :, c0 * CH : c1 * CH]
+            base = 2 if (a, h, 2) in x_raw and c0 >= 2 else 0
+            src = x_raw[a, h, base][:, :, (c0 - base) * CH : (c1 - base) * CH]
             o = g[:].rearrange("p (c i j) -> p c j i", i=4, j=PACK)
             s = src.rearrange("p j (c i) -> p c j i", i=4)
             if eng == "v":
@@ -87,13 +87,13 @@ def tile_mix_cross_none_kernel(tc, x, wb_words, wb_scales, dn_words, dn_scales, 
 
         def h_mm(a, h, ch):
             if a == 0:
-                hbank[h, ch] = ps.tile([P, PACK, CH], F32, name="bank_a%d" % ch)
+                hbank[h, ch] = ps.tile([P, PACK, CH], F32, name=("bank_a%d" if h == 0 else "bank_b%d") % ch)
             cols = slice(ch * CH, (ch + 1) * CH)
             for j in range(PACK):
                 nc.tensor.matmul_mx(
                     out=hbank[h, ch][:, j, :],
                     lhsT=dn_w[a][:, j * P : (j + 1) * P].bitcast(FP8X4),
-                    lhsT_scale=dn_s[a][:, j * P : (j + 1) * P],
+                    lhsT_scale=dn_s[4 * a : P, j * P : (j + 1) * P],
                     rhs=xq[a, h][:, cols].bitcast(FP8X4),
                     rhs_scale=xs[a, h][:, cols],
                     start=(a == 0 and j == 0),
@@ -101,17 +101,18 @@ def tile_mix_cross_none_kernel(tc, x, wb_words, wb_scales, dn_words, dn_scales, 
                 )
 
         def h_copy(h, ch):
-            g = tl("hg%d%d" % (h, ch), [P, CH * PACK], BF16)
-            hg[h, ch] = g
-            nc.scalar.copy(out=g[:].rearrange("p (t j) -> p t j", j=PACK), in_=hbank[h, ch][:].rearrange("p j t -> p t j"))
+            if ch % 2 == 0:
+                hg[h, ch // 2] = tl("hg%d%d" % (h, ch), [P, 2 * CH * PACK], BF16)
+            g = hg[h, ch // 2][:, (ch % 2) * CH * PACK : (ch % 2 + 1) * CH * PACK]
+            nc.scalar.copy(out=g.rearrange("p (t j) -> p t j", j=PACK), in_=hbank[h, ch][:].rearrange("p j t -> p t j"))
 
-        def quant_h(h, ch):
-            cols = slice(ch * CH, (ch + 1) * CH)
-            nc.vector.quantize_mx(out=hq[h][:, cols].bitcast(FP8X4), scales=hs[h][:, cols], in_=hg[h, ch][:])
+        def quant_h(h, c0, c1):
+            cols = slice(c0 * CH, c1 * CH)
+            nc.vector.quantize_mx(out=hq[h][:, cols].bitcast(FP8X4), scales=hs[h][:, cols], in_=hg[h, c0 // 2][:])
 
         def y_wb(a, h, c):
             if a == 0:
-                ybank[h, c] = ps.tile([P, HALF], F32, name=("bank_b%d" if h == 0 else "bank_a%d") % c)
+                ybank[h, c] = ps.tile([P, HALF], F32, name=("bank_a%d" if h == 0 else "bank_b%d") % c)
             nc.tensor.matmul_mx(
                 out=ybank[h, c][:],
                 lhsT=wb_w[:, a, 2 * c * P : 2 * (c + 1) * P].bitcast(FP4X4),
@@ -134,126 +135,170 @@ def tile_mix_cross_none_kernel(tc, x, wb_words, wb_scales, dn_words, dn_scales, 
             )
 
         def gate(c, h):
-            cols = slice(h * HALF, (h + 1) * HALF)
             u = tl("prod%d%d" % (c, h), [P, HALF], F32)
             prod[c, h] = u
-            nc.vector.scalar_tensor_tensor(out=u[:], in0=ybank[h, c][:], scalar=b_col[:, c : c + 1], in1=x0_sb[c][:, cols], op0=ADD, op1=MULT)
+            nc.vector.scalar_tensor_tensor(out=u[:], in0=ybank[h, c][:], scalar=b_col[:, c : c + 1], in1=x0_sb[c, h], op0=ADD, op1=MULT)
 
         def resid(c, h):
             cols = slice(h * HALF, (h + 1) * HALF)
-            nc.vector.tensor_tensor(out=res[c][:, cols], in0=prod[c, h][:], in1=xr_sb[c][:, cols], op=ADD)
+            nc.vector.tensor_tensor(out=res[c][:, cols], in0=prod[c, h][:], in1=xr_sb[c, h], op=ADD)
+
+        def yw(h, c):
+            y_wb(0, h, c)
+            y_wb(1, h, c)
+
+        def store_half(c, h):
+            cols = slice(h * HALF, (h + 1) * HALF)
+            nc.sync.dma_start(out=out[c * P : (c + 1) * P, cols], in_=res[c][:, cols])
+
+        def perm_words(a):
+            nc.vector.tensor_copy(
+                out=dn_w[a][:].rearrange("p (j mo mi) -> p mo j mi", j=PACK, mi=4),
+                in_=dn_raw[:, a, :].rearrange("p (mo mi j) -> p mo j mi", j=PACK, mi=4),
+            )
+
+        def perm_s():
+            nc.vector.tensor_copy(
+                out=dn_s[:].rearrange("p (j mo mi) -> p mo j mi", j=PACK, mi=16),
+                in_=dn_sraw[:].rearrange("p (mo mi j) -> p mo j mi", j=PACK, mi=16),
+            )
+
+        def bias():
+            bt = ps.tile([P, HALF], F32, name="bank_b0")
+            nc.tensor.transpose(bt[:, 0:P], b_rows[:], ident[:])
+            nc.scalar.copy(out=b_col[:], in_=bt[:, 0:NT])
+
+        def prep_x(a, h, on_vector):
+            for ch in range(on_vector):
+                cast("v", a, h, ch, ch + 1)
+            for ch in range(on_vector, NCH):
+                cast("s", a, h, ch, ch + 1)
+            for ch in range(NCH):
+                quant_x(a, h, ch, ch + 1)
+
+        xv = x.rearrange("(a p j) t -> a p j t", p=P, j=PACK)
+
+        def load_x(a, h, c0=0, c1=NCH):
+            nc.sync.dma_start(out=x_raw[a, h, c0][:], in_=xv[a][:, :, h * HALF + c0 * CH : h * HALF + c1 * CH])
+
+        def load_pair_half(name, dst, src, h):
+            t = tl("%s_pair%d" % (name, h), [P, 2, HALF], F32)
+            nc.sync.dma_start(out=t[:], in_=src[0 : 2 * P, h * HALF : (h + 1) * HALF].rearrange("(c p) t -> p c t", p=P))
+            for c in range(2):
+                dst[c, h] = t[:, c, :]
+
+        def load_rows(name, dst, src, c):
+            t = tl("%s_rows%d" % (name, c), [P, T], F32)
+            nc.sync.dma_start(out=t[:], in_=src[c * P : (c + 1) * P, :])
+            for h in range(2):
+                dst[c, h] = t[:, h * HALF : (h + 1) * HALF]
 
         def store(c):
             nc.sync.dma_start(out=out[c * P : (c + 1) * P, :], in_=res[c][:])
 
-        zero(nc.vector, dn_sraw)
+        nc.vector.memset(dn_sraw[:].bitcast(I32), 0)
         zero(nc.vector, wb_s)
         zero(nc.vector, up_s)
         nc.gpsimd.memset(b_rows[:], 0.0)
         make_identity(nc, ident[:])
 
-        xv = x.rearrange("(a p j) t -> a p j t", p=P, j=PACK)
         nc.sync.dma_start(out=dn_raw[:], in_=dn_words.rearrange("a p r i -> p a (r i)").bitcast(I32))
-        load_scales(nc.scalar, dn_sraw, dn_scales, range(4))
-        nc.scalar.dma_start(out=b_rows[0:NT, :], in_=b.rearrange("(c p) -> c p", p=P))
-        load_scales(nc.scalar, wb_s, wb_scales, range(1))
-        nc.sync.dma_start(out=x_first[:], in_=xv[0])
+        load_x(0, 0)
+        nc.sync.dma_start(out=b_rows[0:NT, :], in_=b.rearrange("(c p) -> c p", p=P))
+        for q in range(4):
+            nc.sync.dma_start(out=dn_sraw[32 * q : 32 * q + 8, :].bitcast(I32), in_=dn_scales[:, 4 * q : 4 * q + 4, :].bitcast(I32))
+        load_x(1, 0)
+        load_scales(nc.sync, wb_s, wb_scales, range(4))
         nc.sync.dma_start(out=wb_w[:].bitcast(I32), in_=wb_words.rearrange("a p n -> p a n").bitcast(I32))
-        load_scales(nc.scalar, wb_s, wb_scales, range(1, 4))
-        load_scales(nc.scalar, up_s, upw_scales, range(1))
-        nc.sync.dma_start(out=x_second[0][:], in_=xv[1][:, :, 0:HALF])
-        load_scales(nc.scalar, up_s, upw_scales, range(1, 2))
-        nc.sync.dma_start(out=x_second[1][:], in_=xv[1][:, :, HALF:T])
+        load_x(0, 1)
+        load_scales(nc.sync, up_s, upw_scales, range(2))
+        load_x(1, 1, 0, 2)
+        load_scales(nc.sync, up_s, upw_scales, range(2, 4))
+        load_x(1, 1, 2, 4)
         nc.sync.dma_start(out=up_w[:], in_=upw_words[0].rearrange("p n i -> p (n i)").bitcast(I32))
-        load_scales(nc.scalar, up_s, upw_scales, range(2, 4))
-        for c in range(NT):
-            nc.sync.dma_start(out=x0_sb[c][:], in_=x0[c * P : (c + 1) * P, :])
-            nc.sync.dma_start(out=xr_sb[c][:], in_=xr[c * P : (c + 1) * P, :])
-
-        for a in range(PASSES):
-            nc.vector.tensor_copy(
-                out=dn_w[a][:].rearrange("p (j mo mi) -> p mo j mi", j=PACK, mi=4),
-                in_=dn_raw[:, a, :].rearrange("p (mo mi j) -> p mo j mi", j=PACK, mi=4),
-            )
-        for a in range(PASSES):
-            nc.vector.tensor_copy(
-                out=dn_s[a][:].rearrange("p (j m) -> p m j", j=PACK),
-                in_=dn_sraw[:, a, :].rearrange("p (m j) -> p m j", j=PACK),
-            )
-
-        bt = ps.tile([P, HALF], F32, name="bank_b0")
-        nc.tensor.transpose(bt[:, 0:P], b_rows[:], ident[:])
-        nc.scalar.copy(out=b_col[:], in_=bt[:, 0:NT])
-
-        cast("v", 0, 0, 0, 2)
-        cast("s", 0, 0, 2, 4)
-        cast("v", 0, 1, 0, 2)
-        quant_x(0, 0, 0, 2)
-        quant_x(0, 0, 2, 4)
-        cast("s", 0, 1, 2, 4)
-        quant_x(0, 1, 0, 2)
-        for ch in range(NCH):
-            h_mm(0, 0, ch)
-        for c in range(NT):
-            y_wb(0, 0, c)
-        quant_x(0, 1, 2, 4)
-
-        def second_pass(h):
-            cast("s", 1, h, 3, 4)
-            cast("v", 1, h, 0, 1)
-            cast("v", 1, h, 1, 2)
-            quant_x(1, h, 0, 1)
-            cast("v", 1, h, 2, 3)
-            quant_x(1, h, 1, 2)
-            quant_x(1, h, 3, 4)
-            quant_x(1, h, 2, 3)
-
-        order = [0, 1, 3, 2]
-        second_pass(0)
-        for ch in order:
-            h_mm(1, 0, ch)
-            h_copy(0, ch)
-        for c in range(NT):
-            y_wb(1, 0, c)
-        for ch in order:
-            quant_h(0, ch)
-            h_mm(0, 1, ch)
-        second_pass(1)
-        for c in range(NT):
-            y_up(0, c)
-        for ch in order:
-            h_mm(1, 1, ch)
-            h_copy(1, ch)
-        gate(0, 0)
-        quant_h(1, 0)
-        resid(0, 0)
-        quant_h(1, 1)
-        quant_h(1, 3)
-        quant_h(1, 2)
-        for c in (0, 1):
-            y_wb(0, 1, c)
-            y_wb(1, 1, c)
-        for c in (0, 1):
-            y_up(1, c)
-        for c in (2, 3):
-            y_wb(0, 1, c)
-            y_wb(1, 1, c)
-            y_up(1, c)
-        gate(1, 0)
-        gate(0, 1)
-        resid(1, 0)
-        resid(0, 1)
+        for h in range(2):
+            load_pair_half("x0", x0_sb, x0, h)
+            load_pair_half("xr", xr_sb, xr, h)
+        for c in range(2, NT):
+            load_rows("x0", x0_sb, x0, c)
+            load_rows("xr", xr_sb, xr, c)
+        perm_words(0)
+        perm_words(1)
+        cast("v",0,0,0,1)
+        cast("v",0,0,1,2)
+        cast("s",0,0,2,3)
+        cast("s",0,0,3,4)
+        perm_s()
+        for ch in range(4):
+            quant_x(0,0,ch,ch+1)
+        bias()
+        for ch in range(4):
+            h_mm(0,0,ch)
+        prep_x(1,0,2)
+        for ch in range(4):
+            h_mm(1,0,ch)
+            h_copy(0,ch)
+        yw(0,0)
+        yw(0,1)
+        quant_h(0,0,2)
+        cast("v",0,1,0,1)
+        cast("v",0,1,1,2)
+        quant_x(0,1,0,1)
+        cast("v",0,1,2,3)
+        quant_x(0,1,1,2)
+        cast("s",0,1,3,4)
+        quant_x(0,1,2,3)
+        quant_h(0,2,4)
+        quant_x(0,1,3,4)
+        for ch in range(4):
+            h_mm(0,1,ch)
+        cast("v",1,1,0,1)
+        cast("s",1,1,1,2)
+        cast("s",1,1,2,3)
+        quant_x(1,1,1,2)
+        quant_x(1,1,0,1)
+        cast("v",1,1,3,4)
+        quant_x(1,1,2,3)
+        quant_x(1,1,3,4)
+        h_mm(1,1,0)
+        h_copy(1,0)
+        h_mm(1,1,1)
+        h_copy(1,1)
+        y_up(0,0)
+        h_mm(1,1,2)
+        h_copy(1,2)
+        h_mm(1,1,3)
+        h_copy(1,3)
+        y_up(0,1)
+        gate(0,0)
+        quant_h(1,0,2)
+        gate(1,0)
+        resid(0,0)
+        quant_h(1,2,4)
+        resid(1,0)
+        yw(1,0)
+        yw(1,1)
+        y_up(1,0)
+        y_up(1,1)
+        for c in (2,3):
+            yw(0,c)
+            y_up(0,c)
+            yw(1,c)
+            y_up(1,c)
+        gate(0,1)
+        gate(1,1)
+        resid(0,1)
         store(0)
-        gate(1, 1)
-        gate(2, 0)
-        resid(1, 1)
+        resid(1,1)
         store(1)
-        gate(2, 1)
-        resid(2, 0)
-        gate(3, 0)
-        resid(2, 1)
+        gate(2,0)
+        gate(2,1)
+        resid(2,0)
+        resid(2,1)
         store(2)
-        gate(3, 1)
-        resid(3, 0)
-        resid(3, 1)
-        store(3)
+        gate(3,0)
+        gate(3,1)
+        resid(3,0)
+        store_half(3,0)
+        resid(3,1)
+        store_half(3,1)

@@ -45,11 +45,8 @@ def tile_mix_cross_none_kernel(tc, x, wb_words, wb_scales, dn_words, dn_scales, 
         b_rows = tl("b_rows", [P, P], F32)
         b_col = tl("b_col", [P, NT], F32)
         ident = tl("ident", [P, P], F32)
-        x_raw = {}
-        for a, h in ((0, 0), (1, 0), (0, 1)):
-            x_raw[a, h, 0] = tl("x_raw%d%d" % (a, h), [P, PACK, HALF], F32)
-        for c0 in (0, 2):
-            x_raw[1, 1, c0] = tl("x_raw11%d" % c0, [P, PACK, 2 * CH], F32)
+        x_first = tl("x_first", [P, PACK, T], F32)
+        x_second = [tl("x_second%d" % h, [P, PACK, HALF], F32) for h in range(2)]
         xq = {(a, h): tl("xq%d%d" % (a, h), [P, HALF], I32) for a in range(2) for h in range(2)}
         xs = {(a, h): tl("xs%d%d" % (a, h), [P, HALF], U8) for a in range(2) for h in range(2)}
         hq = [tl("hq%d" % h, [P, HALF], I32) for h in range(2)]
@@ -72,8 +69,10 @@ def tile_mix_cross_none_kernel(tc, x, wb_words, wb_scales, dn_words, dn_scales, 
             w = (c1 - c0) * CH
             g = tl("xg%d%d%d" % (a, h, c0), [P, w * PACK], BF16)
             xg[a, h, c0] = g
-            base = 2 if (a, h, 2) in x_raw and c0 >= 2 else 0
-            src = x_raw[a, h, base][:, :, (c0 - base) * CH : (c1 - base) * CH]
+            if a == 0:
+                src = x_first[:, :, h * HALF + c0 * CH : h * HALF + c1 * CH]
+            else:
+                src = x_second[h][:, :, c0 * CH : c1 * CH]
             o = g[:].rearrange("p (c i j) -> p c j i", i=4, j=PACK)
             s = src.rearrange("p j (c i) -> p c j i", i=4)
             if eng == "v":
@@ -100,11 +99,16 @@ def tile_mix_cross_none_kernel(tc, x, wb_words, wb_scales, dn_words, dn_scales, 
                     stop=(a == PASSES - 1 and j == PACK - 1),
                 )
 
-        def h_copy(h, ch):
+        def h_copy(h, ch, eng="s"):
             if ch % 2 == 0:
                 hg[h, ch // 2] = tl("hg%d%d" % (h, ch), [P, 2 * CH * PACK], BF16)
             g = hg[h, ch // 2][:, (ch % 2) * CH * PACK : (ch % 2 + 1) * CH * PACK]
-            nc.scalar.copy(out=g.rearrange("p (t j) -> p t j", j=PACK), in_=hbank[h, ch][:].rearrange("p j t -> p t j"))
+            o = g.rearrange("p (t j) -> p t j", j=PACK)
+            s = hbank[h, ch][:].rearrange("p j t -> p t j")
+            if eng == "v":
+                nc.vector.tensor_copy(out=o, in_=s)
+            else:
+                nc.scalar.copy(out=o, in_=s)
 
         def quant_h(h, c0, c1):
             cols = slice(c0 * CH, c1 * CH)
@@ -139,9 +143,10 @@ def tile_mix_cross_none_kernel(tc, x, wb_words, wb_scales, dn_words, dn_scales, 
             prod[c, h] = u
             nc.vector.scalar_tensor_tensor(out=u[:], in0=ybank[h, c][:], scalar=b_col[:, c : c + 1], in1=x0_sb[c, h], op0=ADD, op1=MULT)
 
-        def resid(c, h):
+        def resid(c, h, eng="V"):
             cols = slice(h * HALF, (h + 1) * HALF)
-            nc.vector.tensor_tensor(out=res[c][:, cols], in0=prod[c, h][:], in1=xr_sb[c, h], op=ADD)
+            e = nc.vector if eng == "V" else nc.gpsimd
+            e.tensor_tensor(out=res[c][:, cols], in0=prod[c, h][:], in1=xr_sb[c, h], op=ADD)
 
         def yw(h, c):
             y_wb(0, h, c)
@@ -178,15 +183,6 @@ def tile_mix_cross_none_kernel(tc, x, wb_words, wb_scales, dn_words, dn_scales, 
 
         xv = x.rearrange("(a p j) t -> a p j t", p=P, j=PACK)
 
-        def load_x(a, h, c0=0, c1=NCH):
-            nc.sync.dma_start(out=x_raw[a, h, c0][:], in_=xv[a][:, :, h * HALF + c0 * CH : h * HALF + c1 * CH])
-
-        def load_pair_half(name, dst, src, h):
-            t = tl("%s_pair%d" % (name, h), [P, 2, HALF], F32)
-            nc.sync.dma_start(out=t[:], in_=src[0 : 2 * P, h * HALF : (h + 1) * HALF].rearrange("(c p) t -> p c t", p=P))
-            for c in range(2):
-                dst[c, h] = t[:, c, :]
-
         def load_rows(name, dst, src, c):
             t = tl("%s_rows%d" % (name, c), [P, T], F32)
             nc.sync.dma_start(out=t[:], in_=src[c * P : (c + 1) * P, :])
@@ -202,99 +198,92 @@ def tile_mix_cross_none_kernel(tc, x, wb_words, wb_scales, dn_words, dn_scales, 
         nc.gpsimd.memset(b_rows[:], 0.0)
         make_identity(nc, ident[:])
 
+        nc.sync.dma_start(out=x_first[:], in_=xv[0])
         nc.sync.dma_start(out=dn_raw[:], in_=dn_words.rearrange("a p r i -> p a (r i)").bitcast(I32))
-        load_x(0, 0)
         nc.sync.dma_start(out=b_rows[0:NT, :], in_=b.rearrange("(c p) -> c p", p=P))
         for q in range(4):
             nc.sync.dma_start(out=dn_sraw[32 * q : 32 * q + 8, :].bitcast(I32), in_=dn_scales[:, 4 * q : 4 * q + 4, :].bitcast(I32))
-        load_x(1, 0)
+        nc.sync.dma_start(out=x_second[0][:], in_=xv[1][:, :, 0:HALF])
         load_scales(nc.sync, wb_s, wb_scales, range(4))
         nc.sync.dma_start(out=wb_w[:].bitcast(I32), in_=wb_words.rearrange("a p n -> p a n").bitcast(I32))
-        load_x(0, 1)
-        load_scales(nc.sync, up_s, upw_scales, range(2))
-        load_x(1, 1, 0, 2)
-        load_scales(nc.sync, up_s, upw_scales, range(2, 4))
-        load_x(1, 1, 2, 4)
+        nc.sync.dma_start(out=x_second[1][:], in_=xv[1][:, :, HALF:T])
+        load_scales(nc.sync, up_s, upw_scales, range(4))
         nc.sync.dma_start(out=up_w[:], in_=upw_words[0].rearrange("p n i -> p (n i)").bitcast(I32))
-        for h in range(2):
-            load_pair_half("x0", x0_sb, x0, h)
-            load_pair_half("xr", xr_sb, xr, h)
-        for c in range(2, NT):
+        for c in range(NT):
             load_rows("x0", x0_sb, x0, c)
             load_rows("xr", xr_sb, xr, c)
+        cast("v",0,0,0,2)
+        cast("s",0,0,2,4)
+        cast("v",0,1,0,2)
+        cast("s",0,1,2,4)
+        quant_x(0,0,0,2)
         perm_words(0)
-        perm_words(1)
-        cast("v",0,0,0,1)
-        cast("v",0,0,1,2)
-        cast("s",0,0,2,3)
-        cast("s",0,0,3,4)
         perm_s()
-        for ch in range(4):
-            quant_x(0,0,ch,ch+1)
+        quant_x(0,0,2,4)
+        perm_words(1)
         bias()
+        quant_x(0,1,0,2)
+        quant_x(0,1,2,4)
         for ch in range(4):
             h_mm(0,0,ch)
+        h_mm(0,1,0)
+        h_mm(0,1,1)
         prep_x(1,0,2)
         for ch in range(4):
             h_mm(1,0,ch)
             h_copy(0,ch)
+        h_mm(0,1,2)
+        h_mm(0,1,3)
         yw(0,0)
         yw(0,1)
+        yw(0,2)
         quant_h(0,0,2)
-        cast("v",0,1,0,1)
-        cast("v",0,1,1,2)
-        quant_x(0,1,0,1)
-        cast("v",0,1,2,3)
-        quant_x(0,1,1,2)
-        cast("s",0,1,3,4)
-        quant_x(0,1,2,3)
-        quant_h(0,2,4)
-        quant_x(0,1,3,4)
-        for ch in range(4):
-            h_mm(0,1,ch)
         cast("v",1,1,0,1)
-        cast("s",1,1,1,2)
+        cast("v",1,1,1,2)
         cast("s",1,1,2,3)
-        quant_x(1,1,1,2)
+        cast("s",1,1,3,4)
         quant_x(1,1,0,1)
-        cast("v",1,1,3,4)
+        quant_x(1,1,1,2)
+        quant_h(0,2,4)
         quant_x(1,1,2,3)
         quant_x(1,1,3,4)
         h_mm(1,1,0)
         h_copy(1,0)
         h_mm(1,1,1)
-        h_copy(1,1)
-        y_up(0,0)
+        h_copy(1,1,"v")
         h_mm(1,1,2)
         h_copy(1,2)
         h_mm(1,1,3)
-        h_copy(1,3)
+        h_copy(1,3,"v")
+        y_up(0,0)
         y_up(0,1)
-        gate(0,0)
         quant_h(1,0,2)
-        gate(1,0)
-        resid(0,0)
         quant_h(1,2,4)
-        resid(1,0)
+        gate(0,0)
         yw(1,0)
         yw(1,1)
         y_up(1,0)
         y_up(1,1)
-        for c in (2,3):
-            yw(0,c)
-            y_up(0,c)
-            yw(1,c)
-            y_up(1,c)
+        y_up(0,2)
+        yw(1,2)
+        y_up(1,2)
+        yw(0,3)
+        y_up(0,3)
+        yw(1,3)
+        y_up(1,3)
         gate(0,1)
-        gate(1,1)
-        resid(0,1)
+        resid(0,0)
+        resid(0,1,"G")
         store(0)
-        resid(1,1)
+        gate(1,0)
+        gate(1,1)
+        resid(1,0)
+        resid(1,1,"G")
         store(1)
         gate(2,0)
         gate(2,1)
         resid(2,0)
-        resid(2,1)
+        resid(2,1,"G")
         store(2)
         gate(3,0)
         gate(3,1)

@@ -1,7 +1,6 @@
 from contextlib import ExitStack
 
 import concourse.mybir as mybir
-from concourse.masks import make_identity
 
 K, R, N, T = 1024, 512, 512, 1024
 FLOPS = 2 * T * (K * R + K * N + R * N)
@@ -43,10 +42,10 @@ def tile_mix_cross_none_kernel(tc, x, wb_words, wb_scales, dn_words, dn_scales, 
         up_w = tl("up_w", [P, N], I32)
         up_s = tl("up_s", [P, 1, N], U8)
         b_rows = tl("b_rows", [P, P], F32)
-        b_col = tl("b_col", [P, NT], F32)
-        ident = tl("ident", [P, P], F32)
+        b_t = tl("b_t", [P, P], F32)
         x_first = tl("x_first", [P, PACK, T], F32)
-        x_second = [tl("x_second%d" % h, [P, PACK, HALF], F32) for h in range(2)]
+        x_pair = [tl("x_pair%d" % u, [P, 2, T], F32) for u in range(2)]
+        xg_last = [tl("xg_last%d" % h, [P, HALF * PACK], BF16) for h in range(2)]
         xq = {(a, h): tl("xq%d%d" % (a, h), [P, HALF], I32) for a in range(2) for h in range(2)}
         xs = {(a, h): tl("xs%d%d" % (a, h), [P, HALF], U8) for a in range(2) for h in range(2)}
         hq = [tl("hq%d" % h, [P, HALF], I32) for h in range(2)]
@@ -69,10 +68,7 @@ def tile_mix_cross_none_kernel(tc, x, wb_words, wb_scales, dn_words, dn_scales, 
             w = (c1 - c0) * CH
             g = tl("xg%d%d%d" % (a, h, c0), [P, w * PACK], BF16)
             xg[a, h, c0] = g
-            if a == 0:
-                src = x_first[:, :, h * HALF + c0 * CH : h * HALF + c1 * CH]
-            else:
-                src = x_second[h][:, :, c0 * CH : c1 * CH]
+            src = x_first[:, :, h * HALF + c0 * CH : h * HALF + c1 * CH]
             o = g[:].rearrange("p (c i j) -> p c j i", i=4, j=PACK)
             s = src.rearrange("p j (c i) -> p c j i", i=4)
             if eng == "v":
@@ -80,13 +76,23 @@ def tile_mix_cross_none_kernel(tc, x, wb_words, wb_scales, dn_words, dn_scales, 
             else:
                 nc.scalar.copy(out=o, in_=s)
 
+        def cast_pair(eng, u, h, c0, c1):
+            g = xg_last[h][:, c0 * CH * PACK : c1 * CH * PACK]
+            o = g.rearrange("p (t j) -> p t j", j=PACK)[:, :, 2 * u : 2 * u + 2]
+            s = x_pair[u][:, :, h * HALF + c0 * CH : h * HALF + c1 * CH].rearrange("p j t -> p t j")
+            if eng == "v":
+                nc.vector.tensor_copy(out=o, in_=s)
+            else:
+                nc.scalar.copy(out=o, in_=s)
+
         def quant_x(a, h, c0, c1):
             cols = slice(c0 * CH, c1 * CH)
-            nc.vector.quantize_mx(out=xq[a, h][:, cols].bitcast(FP8X4), scales=xs[a, h][:, cols], in_=xg[a, h, c0][:])
+            g = xg[a, h, c0][:] if a == 0 else xg_last[h][:, c0 * CH * PACK : c1 * CH * PACK]
+            nc.vector.quantize_mx(out=xq[a, h][:, cols].bitcast(FP8X4), scales=xs[a, h][:, cols], in_=g)
 
         def h_mm(a, h, ch):
             if a == 0:
-                hbank[h, ch] = ps.tile([P, PACK, CH], F32, name=("bank_a%d" if h == 0 else "bank_b%d") % ch)
+                hbank[h, ch] = ps.tile([P, PACK, CH], F32, name="bank%d" % (NCH * h + ch))
             cols = slice(ch * CH, (ch + 1) * CH)
             for j in range(PACK):
                 nc.tensor.matmul_mx(
@@ -116,7 +122,7 @@ def tile_mix_cross_none_kernel(tc, x, wb_words, wb_scales, dn_words, dn_scales, 
 
         def y_wb(a, h, c):
             if a == 0:
-                ybank[h, c] = ps.tile([P, HALF], F32, name=("bank_a%d" if h == 0 else "bank_b%d") % c)
+                ybank[h, c] = ps.tile([P, HALF], F32, name="bank%d" % (2 * c + h))
             nc.tensor.matmul_mx(
                 out=ybank[h, c][:],
                 lhsT=wb_w[:, a, 2 * c * P : 2 * (c + 1) * P].bitcast(FP4X4),
@@ -141,7 +147,7 @@ def tile_mix_cross_none_kernel(tc, x, wb_words, wb_scales, dn_words, dn_scales, 
         def gate(c, h):
             u = tl("prod%d%d" % (c, h), [P, HALF], F32)
             prod[c, h] = u
-            nc.vector.scalar_tensor_tensor(out=u[:], in0=ybank[h, c][:], scalar=b_col[:, c : c + 1], in1=x0_sb[c, h], op0=ADD, op1=MULT)
+            nc.vector.scalar_tensor_tensor(out=u[:], in0=ybank[h, c][:], scalar=b_t[:, 32 * c : 32 * c + 1], in1=x0_sb[c, h], op0=ADD, op1=MULT)
 
         def resid(c, h, eng="V"):
             cols = slice(h * HALF, (h + 1) * HALF)
@@ -169,9 +175,7 @@ def tile_mix_cross_none_kernel(tc, x, wb_words, wb_scales, dn_words, dn_scales, 
             )
 
         def bias():
-            bt = ps.tile([P, HALF], F32, name="bank_b0")
-            nc.tensor.transpose(bt[:, 0:P], b_rows[:], ident[:])
-            nc.scalar.copy(out=b_col[:], in_=bt[:, 0:NT])
+            nc.vector.transpose(b_t[:], b_rows[:])
 
         def prep_x(a, h, on_vector):
             for ch in range(on_vector):
@@ -183,11 +187,12 @@ def tile_mix_cross_none_kernel(tc, x, wb_words, wb_scales, dn_words, dn_scales, 
 
         xv = x.rearrange("(a p j) t -> a p j t", p=P, j=PACK)
 
-        def load_rows(name, dst, src, c):
-            t = tl("%s_rows%d" % (name, c), [P, T], F32)
-            nc.sync.dma_start(out=t[:], in_=src[c * P : (c + 1) * P, :])
-            for h in range(2):
-                dst[c, h] = t[:, h * HALF : (h + 1) * HALF]
+        def load_rows(name, dst, src, c0, c1):
+            t = tl("%s_rows%d" % (name, c0), [P, c1 - c0, T], F32)
+            nc.sync.dma_start(out=t[:], in_=src[c0 * P : c1 * P, :].rearrange("(c p) t -> p c t", p=P))
+            for c in range(c0, c1):
+                for h in range(2):
+                    dst[c, h] = t[:, c - c0, h * HALF : (h + 1) * HALF]
 
         def store(c):
             nc.sync.dma_start(out=out[c * P : (c + 1) * P, :], in_=res[c][:])
@@ -196,98 +201,104 @@ def tile_mix_cross_none_kernel(tc, x, wb_words, wb_scales, dn_words, dn_scales, 
         zero(nc.vector, wb_s)
         zero(nc.vector, up_s)
         nc.gpsimd.memset(b_rows[:], 0.0)
-        make_identity(nc, ident[:])
 
         nc.sync.dma_start(out=x_first[:], in_=xv[0])
-        nc.sync.dma_start(out=dn_raw[:], in_=dn_words.rearrange("a p r i -> p a (r i)").bitcast(I32))
-        nc.sync.dma_start(out=b_rows[0:NT, :], in_=b.rearrange("(c p) -> c p", p=P))
         for q in range(4):
             nc.sync.dma_start(out=dn_sraw[32 * q : 32 * q + 8, :].bitcast(I32), in_=dn_scales[:, 4 * q : 4 * q + 4, :].bitcast(I32))
-        nc.sync.dma_start(out=x_second[0][:], in_=xv[1][:, :, 0:HALF])
+        nc.sync.dma_start(out=dn_raw[:], in_=dn_words.rearrange("a p r i -> p a (r i)").bitcast(I32))
+        for u in range(2):
+            nc.sync.dma_start(out=x_pair[u][:], in_=xv[1][:, 2 * u : 2 * u + 2, :])
         load_scales(nc.sync, wb_s, wb_scales, range(4))
         nc.sync.dma_start(out=wb_w[:].bitcast(I32), in_=wb_words.rearrange("a p n -> p a n").bitcast(I32))
-        nc.sync.dma_start(out=x_second[1][:], in_=xv[1][:, :, HALF:T])
-        load_scales(nc.sync, up_s, upw_scales, range(4))
         nc.sync.dma_start(out=up_w[:], in_=upw_words[0].rearrange("p n i -> p (n i)").bitcast(I32))
-        for c in range(NT):
-            load_rows("x0", x0_sb, x0, c)
-            load_rows("xr", xr_sb, xr, c)
-        cast("v",0,0,0,2)
-        cast("s",0,0,2,4)
-        cast("v",0,1,0,2)
-        cast("s",0,1,2,4)
-        quant_x(0,0,0,2)
-        perm_words(0)
+        load_rows("x0", x0_sb, x0, 0, 2)
+        load_scales(nc.sync, up_s, upw_scales, range(4))
+        nc.sync.dma_start(out=b_rows[0:P:32, :].rearrange("q (c i) -> q c i", i=32), in_=b.rearrange("(c q i) -> q c i", q=4, i=32))
+        load_rows("xr", xr_sb, xr, 0, 1)
+        load_rows("xr", xr_sb, xr, 1, 2)
+        for c in range(2, NT):
+            load_rows("x0", x0_sb, x0, c, c + 1)
+            load_rows("xr", xr_sb, xr, c, c + 1)
+
+        cast("v", 0, 0, 0, 2)
+        cast("s", 0, 0, 2, 4)
         perm_s()
-        quant_x(0,0,2,4)
+        quant_x(0, 0, 0, 2)
+        cast("s", 0, 1, 2, 4)
+        perm_words(0)
+        quant_x(0, 0, 2, 4)
+        cast("v", 0, 1, 0, 2)
         perm_words(1)
+        quant_x(0, 1, 0, 2)
+        cast_pair("v", 0, 0, 0, 4)
+        cast_pair("s", 0, 1, 2, 4)
+        quant_x(0, 1, 2, 4)
+        cast_pair("v", 0, 1, 0, 2)
+        for h in range(2):
+            for ch in range(NCH):
+                h_mm(0, h, ch)
+
+        cast_pair("v", 1, 0, 0, 1)
+        cast_pair("s", 1, 0, 2, 3)
+        cast_pair("v", 1, 0, 1, 2)
+        cast_pair("s", 1, 1, 0, 1)
+        cast_pair("s", 1, 1, 2, 3)
+        quant_x(1, 0, 0, 1)
+        cast_pair("v", 1, 0, 3, 4)
+        quant_x(1, 0, 1, 2)
+        quant_x(1, 0, 2, 3)
+        cast_pair("v", 1, 1, 1, 2)
+        quant_x(1, 0, 3, 4)
+        quant_x(1, 1, 0, 1)
+        cast_pair("v", 1, 1, 3, 4)
+        quant_x(1, 1, 1, 2)
+        quant_x(1, 1, 2, 4)
+        for h in range(2):
+            for ch in range(NCH):
+                h_mm(1, h, ch)
+        h_copy(0, 0)
+        h_copy(0, 1)
+        h_copy(0, 2)
+        h_copy(0, 3, "v")
+        quant_h(0, 0, 2)
+        h_copy(1, 0)
+        h_copy(1, 1)
+        h_copy(1, 2)
+        quant_h(0, 2, 4)
+        h_copy(1, 3, "v")
         bias()
-        quant_x(0,1,0,2)
-        quant_x(0,1,2,4)
-        for ch in range(4):
-            h_mm(0,0,ch)
-        h_mm(0,1,0)
-        h_mm(0,1,1)
-        prep_x(1,0,2)
-        for ch in range(4):
-            h_mm(1,0,ch)
-            h_copy(0,ch)
-        h_mm(0,1,2)
-        h_mm(0,1,3)
-        yw(0,0)
-        yw(0,1)
-        yw(0,2)
-        quant_h(0,0,2)
-        cast("v",1,1,0,1)
-        cast("v",1,1,1,2)
-        cast("s",1,1,2,3)
-        cast("s",1,1,3,4)
-        quant_x(1,1,0,1)
-        quant_x(1,1,1,2)
-        quant_h(0,2,4)
-        quant_x(1,1,2,3)
-        quant_x(1,1,3,4)
-        h_mm(1,1,0)
-        h_copy(1,0)
-        h_mm(1,1,1)
-        h_copy(1,1,"v")
-        h_mm(1,1,2)
-        h_copy(1,2)
-        h_mm(1,1,3)
-        h_copy(1,3,"v")
-        y_up(0,0)
-        y_up(0,1)
-        quant_h(1,0,2)
-        quant_h(1,2,4)
-        gate(0,0)
-        yw(1,0)
-        yw(1,1)
-        y_up(1,0)
-        y_up(1,1)
-        y_up(0,2)
-        yw(1,2)
-        y_up(1,2)
-        yw(0,3)
-        y_up(0,3)
-        yw(1,3)
-        y_up(1,3)
-        gate(0,1)
-        resid(0,0)
-        resid(0,1,"G")
+        yw(0, 0)
+        y_up(0, 0)
+        yw(1, 0)
+        quant_h(1, 0, 2)
+        gate(0, 0)
+        quant_h(1, 2, 4)
+        yw(0, 1)
+        y_up(0, 1)
+        y_up(1, 0)
+        yw(1, 1)
+        y_up(1, 1)
+        for c in range(2, NT):
+            for h in range(2):
+                yw(h, c)
+                y_up(h, c)
+        resid(0, 0)
+        gate(1, 0)
+        resid(1, 0, "G")
+        gate(0, 1)
+        gate(1, 1)
+        resid(0, 1)
         store(0)
-        gate(1,0)
-        gate(1,1)
-        resid(1,0)
-        resid(1,1,"G")
+        resid(1, 1, "G")
         store(1)
-        gate(2,0)
-        gate(2,1)
-        resid(2,0)
-        resid(2,1,"G")
+        gate(2, 0)
+        gate(2, 1)
+        resid(2, 0)
+        resid(2, 1, "G")
         store(2)
-        gate(3,0)
-        gate(3,1)
-        resid(3,0)
-        store_half(3,0)
-        resid(3,1)
-        store_half(3,1)
+        gate(3, 0)
+        gate(3, 1)
+        resid(3, 0)
+        store_half(3, 0)
+        resid(3, 1)
+        store_half(3, 1)

@@ -21,6 +21,8 @@ HALF = 512
 CH = 128
 NCH = HALF // CH
 NT = N // P
+DN_ROW = 4
+UP_ROW = 8
 
 
 def tile_mix_cross_none_kernel(tc, x, wb_words, wb_scales, dn_words, dn_scales, upw_words, upw_scales, x0, b, xr, out):
@@ -34,9 +36,9 @@ def tile_mix_cross_none_kernel(tc, x, wb_words, wb_scales, dn_words, dn_scales, 
             return sb.tile(shape, dtype, name=name, align_bytes=64)
 
         dn_raw = tl("dn_raw", [P, PASSES, R], I32)
-        dn_sraw = tl("dn_sraw", [P, R], U8)
+        dn_sraw = tl("dn_sraw", [P, PASSES, R], U8)
         dn_w = [tl("dn_w%d" % a, [P, R], I32) for a in range(PASSES)]
-        dn_s = tl("dn_s", [P, R], U8)
+        dn_s = tl("dn_s", [P, PASSES, R], U8)
         wb_w = tl("wb_w", [P, PASSES, 2 * N], U8)
         wb_s = tl("wb_s", [P, PASSES, N], U8)
         up_w = tl("up_w", [P, N], I32)
@@ -52,12 +54,13 @@ def tile_mix_cross_none_kernel(tc, x, wb_words, wb_scales, dn_words, dn_scales, 
         hs = [tl("hs%d" % h, [P, HALF], U8) for h in range(2)]
         x0_sb, xr_sb = {}, {}
         res = [tl("res%d" % c, [P, T], F32) for c in range(NT)]
-        xg, hg, prod, hbank, ybank = {}, {}, {}, {}, {}
+        prod = [tl("prod%d" % c, [P, T], F32) for c in range(NT)]
+        xg, hg, hbank, ybank = {}, {}, {}, {}
 
-        def load_scales(eng, plane, scales, quads):
+        def load_scales(eng, plane, scales, quads, row0=0):
             for q in quads:
                 eng.dma_start(
-                    out=plane[32 * q : 32 * q + 4].bitcast(I32),
+                    out=plane[32 * q + row0 : 32 * q + row0 + 4].bitcast(I32),
                     in_=scales[:, 4 * q : 4 * q + 4, :].rearrange("a r n -> r a n").bitcast(I32),
                 )
 
@@ -98,7 +101,7 @@ def tile_mix_cross_none_kernel(tc, x, wb_words, wb_scales, dn_words, dn_scales, 
                 nc.tensor.matmul_mx(
                     out=hbank[h, ch][:, j, :],
                     lhsT=dn_w[a][:, j * P : (j + 1) * P].bitcast(FP8X4),
-                    lhsT_scale=dn_s[4 * a : P, j * P : (j + 1) * P],
+                    lhsT_scale=dn_s[DN_ROW:P, a, j * P : (j + 1) * P],
                     rhs=xq[a, h][:, cols].bitcast(FP8X4),
                     rhs_scale=xs[a, h][:, cols],
                     start=(a == 0 and j == 0),
@@ -137,7 +140,7 @@ def tile_mix_cross_none_kernel(tc, x, wb_words, wb_scales, dn_words, dn_scales, 
             nc.tensor.matmul_mx(
                 out=ybank[h, c][:],
                 lhsT=up_w[:, c * P : (c + 1) * P].bitcast(FP8X4),
-                lhsT_scale=up_s[:, 0, c * P : (c + 1) * P],
+                lhsT_scale=up_s[UP_ROW:P, 0, c * P : (c + 1) * P],
                 rhs=hq[h][:].bitcast(FP8X4),
                 rhs_scale=hs[h][:],
                 start=False,
@@ -145,22 +148,15 @@ def tile_mix_cross_none_kernel(tc, x, wb_words, wb_scales, dn_words, dn_scales, 
             )
 
         def gate(c, h):
-            u = tl("prod%d%d" % (c, h), [P, HALF], F32)
-            prod[c, h] = u
-            nc.vector.scalar_tensor_tensor(out=u[:], in0=ybank[h, c][:], scalar=b_t[:, 32 * c : 32 * c + 1], in1=x0_sb[c, h], op0=ADD, op1=MULT)
-
-        def resid(c, h, eng="V"):
             cols = slice(h * HALF, (h + 1) * HALF)
-            e = nc.vector if eng == "V" else nc.gpsimd
-            e.tensor_tensor(out=res[c][:, cols], in0=prod[c, h][:], in1=xr_sb[c, h], op=ADD)
+            nc.vector.scalar_tensor_tensor(out=prod[c][:, cols], in0=ybank[h, c][:], scalar=b_t[:, 32 * c : 32 * c + 1], in1=x0_sb[c][:, cols], op0=ADD, op1=MULT)
+
+        def resid(e, c, t0, t1):
+            e.tensor_tensor(out=res[c][:, t0:t1], in0=prod[c][:, t0:t1], in1=xr_sb[c][:, t0:t1], op=ADD)
 
         def yw(h, c):
             y_wb(0, h, c)
             y_wb(1, h, c)
-
-        def store_half(c, h):
-            cols = slice(h * HALF, (h + 1) * HALF)
-            nc.sync.dma_start(out=out[c * P : (c + 1) * P, cols], in_=res[c][:, cols])
 
         def perm_words(a):
             nc.vector.tensor_copy(
@@ -168,10 +164,10 @@ def tile_mix_cross_none_kernel(tc, x, wb_words, wb_scales, dn_words, dn_scales, 
                 in_=dn_raw[:, a, :].rearrange("p (mo mi j) -> p mo j mi", j=PACK, mi=4),
             )
 
-        def perm_s():
+        def perm_s(a):
             nc.vector.tensor_copy(
-                out=dn_s[:].rearrange("p (j mo mi) -> p mo j mi", j=PACK, mi=16),
-                in_=dn_sraw[:].rearrange("p (mo mi j) -> p mo j mi", j=PACK, mi=16),
+                out=dn_s[:, a, :].rearrange("p (j mo mi) -> p mo j mi", j=PACK, mi=16),
+                in_=dn_sraw[:, a, :].rearrange("p (mo mi j) -> p mo j mi", j=PACK, mi=16),
             )
 
         def bias():
@@ -191,44 +187,49 @@ def tile_mix_cross_none_kernel(tc, x, wb_words, wb_scales, dn_words, dn_scales, 
             t = tl("%s_rows%d" % (name, c0), [P, c1 - c0, T], F32)
             nc.sync.dma_start(out=t[:], in_=src[c0 * P : c1 * P, :].rearrange("(c p) t -> p c t", p=P))
             for c in range(c0, c1):
-                for h in range(2):
-                    dst[c, h] = t[:, c - c0, h * HALF : (h + 1) * HALF]
+                dst[c] = t[:, c - c0, :]
 
-        def store(c):
-            nc.sync.dma_start(out=out[c * P : (c + 1) * P, :], in_=res[c][:])
+        def store(c, t0=0, t1=T):
+            nc.sync.dma_start(out=out[c * P : (c + 1) * P, t0:t1], in_=res[c][:, t0:t1])
 
-        nc.vector.memset(dn_sraw[:].bitcast(I32), 0)
+        zero(nc.vector, dn_sraw)
         zero(nc.vector, wb_s)
         zero(nc.vector, up_s)
         nc.gpsimd.memset(b_rows[:], 0.0)
 
-        nc.sync.dma_start(out=x_first[:], in_=xv[0])
-        for q in range(4):
-            nc.sync.dma_start(out=dn_sraw[32 * q : 32 * q + 8, :].bitcast(I32), in_=dn_scales[:, 4 * q : 4 * q + 4, :].bitcast(I32))
         nc.sync.dma_start(out=dn_raw[:], in_=dn_words.rearrange("a p r i -> p a (r i)").bitcast(I32))
-        for u in range(2):
-            nc.sync.dma_start(out=x_pair[u][:], in_=xv[1][:, 2 * u : 2 * u + 2, :])
-        load_scales(nc.sync, wb_s, wb_scales, range(4))
+        load_scales(nc.sync, dn_sraw, dn_scales, range(4), DN_ROW)
+        nc.sync.dma_start(out=b_rows[0:P:32, :].rearrange("q (c i) -> q c i", i=32), in_=b.rearrange("(c q i) -> q c i", q=4, i=32))
+        nc.sync.dma_start(out=x_first[:], in_=xv[0])
+        load_scales(nc.sync, wb_s, wb_scales, range(3))
+        nc.sync.dma_start(out=x_pair[0][:], in_=xv[1][:, 0:2, :])
+        load_scales(nc.sync, wb_s, wb_scales, [3])
+        load_scales(nc.sync, up_s, upw_scales, [0], UP_ROW)
+        nc.sync.dma_start(out=x_pair[1][:], in_=xv[1][:, 2:4, :])
         nc.sync.dma_start(out=wb_w[:].bitcast(I32), in_=wb_words.rearrange("a p n -> p a n").bitcast(I32))
         nc.sync.dma_start(out=up_w[:], in_=upw_words[0].rearrange("p n i -> p (n i)").bitcast(I32))
         load_rows("x0", x0_sb, x0, 0, 2)
-        load_scales(nc.sync, up_s, upw_scales, range(4))
-        nc.sync.dma_start(out=b_rows[0:P:32, :].rearrange("q (c i) -> q c i", i=32), in_=b.rearrange("(c q i) -> q c i", q=4, i=32))
+        load_scales(nc.sync, up_s, upw_scales, range(1, 4), UP_ROW)
         load_rows("xr", xr_sb, xr, 0, 1)
         load_rows("xr", xr_sb, xr, 1, 2)
-        for c in range(2, NT):
-            load_rows("x0", x0_sb, x0, c, c + 1)
-            load_rows("xr", xr_sb, xr, c, c + 1)
+        load_rows("x0", x0_sb, x0, 2, 4)
+        load_rows("xr", xr_sb, xr, 2, 3)
+        load_rows("xr", xr_sb, xr, 3, 4)
 
-        cast("v", 0, 0, 0, 2)
+        for a in range(PASSES):
+            perm_words(a)
+        for a in range(PASSES):
+            perm_s(a)
+        bias()
+
+        cast("v", 0, 0, 0, 1)
         cast("s", 0, 0, 2, 4)
-        perm_s()
-        quant_x(0, 0, 0, 2)
+        cast("v", 0, 0, 1, 2)
+        quant_x(0, 0, 0, 1)
         cast("s", 0, 1, 2, 4)
-        perm_words(0)
-        quant_x(0, 0, 2, 4)
+        quant_x(0, 0, 1, 2)
         cast("v", 0, 1, 0, 2)
-        perm_words(1)
+        quant_x(0, 0, 2, 4)
         quant_x(0, 1, 0, 2)
         cast_pair("v", 0, 0, 0, 4)
         cast_pair("s", 0, 1, 2, 4)
@@ -266,39 +267,40 @@ def tile_mix_cross_none_kernel(tc, x, wb_words, wb_scales, dn_words, dn_scales, 
         h_copy(1, 2)
         quant_h(0, 2, 4)
         h_copy(1, 3, "v")
-        bias()
         yw(0, 0)
         y_up(0, 0)
         yw(1, 0)
         quant_h(1, 0, 2)
-        gate(0, 0)
         quant_h(1, 2, 4)
         yw(0, 1)
-        y_up(0, 1)
         y_up(1, 0)
+        y_up(0, 1)
         yw(1, 1)
         y_up(1, 1)
         for c in range(2, NT):
             for h in range(2):
                 yw(h, c)
                 y_up(h, c)
-        resid(0, 0)
-        gate(1, 0)
-        resid(1, 0, "G")
+        gate(0, 0)
+        resid(nc.gpsimd, 0, 0, 512)
         gate(0, 1)
-        gate(1, 1)
-        resid(0, 1)
+        gate(1, 0)
+        resid(nc.vector, 0, 512, T)
         store(0)
-        resid(1, 1, "G")
-        store(1)
+        resid(nc.gpsimd, 1, 0, 448)
+        gate(1, 1)
         gate(2, 0)
+        resid(nc.vector, 1, 448, T)
+        store(1)
+        resid(nc.gpsimd, 2, 0, HALF)
+        store(2, 0, HALF)
         gate(2, 1)
-        resid(2, 0)
-        resid(2, 1, "G")
-        store(2)
         gate(3, 0)
+        resid(nc.vector, 2, HALF, T)
+        store(2, HALF, T)
+        resid(nc.gpsimd, 3, 0, 256)
         gate(3, 1)
-        resid(3, 0)
-        store_half(3, 0)
-        resid(3, 1)
-        store_half(3, 1)
+        resid(nc.vector, 3, 256, HALF)
+        store(3, 0, HALF)
+        resid(nc.vector, 3, HALF, T)
+        store(3, HALF, T)

@@ -192,10 +192,10 @@ def tile_mix_cross_none_kernel(tc, x, wb_words, wb_scales, dn_words, dn_scales, 
         def store(c, t0=0, t1=T):
             nc.sync.dma_start(out=out[c * P : (c + 1) * P, t0:t1], in_=res[c][:, t0:t1])
 
-        zero(nc.vector, dn_sraw)
+        zero(nc.gpsimd, dn_sraw)
+        nc.gpsimd.memset(b_rows[:], 0.0)
         zero(nc.vector, wb_s)
         zero(nc.vector, up_s)
-        nc.gpsimd.memset(b_rows[:], 0.0)
 
         nc.sync.dma_start(out=dn_raw[:], in_=dn_words.rearrange("a p r i -> p a (r i)").bitcast(I32))
         load_scales(nc.sync, dn_sraw, dn_scales, range(4), DN_ROW)
@@ -212,9 +212,9 @@ def tile_mix_cross_none_kernel(tc, x, wb_words, wb_scales, dn_words, dn_scales, 
         load_scales(nc.sync, up_s, upw_scales, range(1, 4), UP_ROW)
         load_rows("xr", xr_sb, xr, 0, 1)
         load_rows("xr", xr_sb, xr, 1, 2)
-        load_rows("x0", x0_sb, x0, 2, 4)
-        load_rows("xr", xr_sb, xr, 2, 3)
-        load_rows("xr", xr_sb, xr, 3, 4)
+        for c in range(2, NT):
+            load_rows("x0", x0_sb, x0, c, c + 1)
+            load_rows("xr", xr_sb, xr, c, c + 1)
 
         for a in range(PASSES):
             perm_words(a)
@@ -243,16 +243,13 @@ def tile_mix_cross_none_kernel(tc, x, wb_words, wb_scales, dn_words, dn_scales, 
         cast_pair("s", 1, 0, 2, 3)
         cast_pair("v", 1, 0, 1, 2)
         cast_pair("s", 1, 1, 0, 1)
-        cast_pair("s", 1, 1, 2, 3)
+        cast_pair("s", 1, 1, 1, 2)
         quant_x(1, 0, 0, 1)
         cast_pair("v", 1, 0, 3, 4)
-        quant_x(1, 0, 1, 2)
-        quant_x(1, 0, 2, 3)
-        cast_pair("v", 1, 1, 1, 2)
+        quant_x(1, 0, 1, 3)
+        cast_pair("v", 1, 1, 2, 4)
         quant_x(1, 0, 3, 4)
-        quant_x(1, 1, 0, 1)
-        cast_pair("v", 1, 1, 3, 4)
-        quant_x(1, 1, 1, 2)
+        quant_x(1, 1, 0, 2)
         quant_x(1, 1, 2, 4)
         for h in range(2):
             for ch in range(NCH):

@@ -8,6 +8,8 @@ FLOPS = 2 * T * (K * R + K * N + R * N)
 F32 = mybir.dt.float32
 BF16 = mybir.dt.bfloat16
 I32 = mybir.dt.int32
+U32 = mybir.dt.uint32
+U16 = mybir.dt.uint16
 U8 = mybir.dt.uint8
 FP8X4 = mybir.dt.float8_e4m3fn_x4
 FP4X4 = mybir.dt.float4_e2m1fn_x4
@@ -21,6 +23,7 @@ HALF = 512
 CH = 128
 NCH = HALF // CH
 NT = N // P
+WB_ROW = 0
 DN_ROW = 4
 UP_ROW = 8
 
@@ -35,62 +38,83 @@ def tile_mix_cross_none_kernel(tc, x, wb_words, wb_scales, dn_words, dn_scales, 
         def tl(name, shape, dtype):
             return sb.tile(shape, dtype, name=name, align_bytes=64)
 
-        dn_raw = tl("dn_raw", [P, PASSES, R], I32)
+        dn_raw = tl("dn_raw", [P, PASSES, R], U32)
+        dn_w = [tl("dn_w%d" % a, [P, R], U32) for a in range(PASSES)]
         dn_sraw = tl("dn_sraw", [P, PASSES, R], U8)
-        dn_w = [tl("dn_w%d" % a, [P, R], I32) for a in range(PASSES)]
         dn_s = tl("dn_s", [P, PASSES, R], U8)
-        wb_w = tl("wb_w", [P, PASSES, 2 * N], U8)
-        wb_s = tl("wb_s", [P, PASSES, N], U8)
-        up_w = tl("up_w", [P, N], I32)
-        up_s = tl("up_s", [P, 1, N], U8)
-        b_rows = tl("b_rows", [P, P], F32)
-        b_t = tl("b_t", [P, P], F32)
+        wb_raw = tl("wb_raw", [P, PASSES, N], U16)
+        wb_w = tl("wb_w", [P, NT, PASSES * P], U16)
+        up_raw = tl("up_raw", [P, N], U32)
+        up_w = tl("up_w", [P, N], U32)
+        y_sraw = tl("y_sraw", [P, PASSES, N], U8)
+        y_s = tl("y_s", [P, PASSES, N], U8)
+        b_sb = tl("b_sb", [P, NT], F32)
         x_first = tl("x_first", [P, PACK, T], F32)
         x_pair = [tl("x_pair%d" % u, [P, 2, T], F32) for u in range(2)]
         xg_last = [tl("xg_last%d" % h, [P, HALF * PACK], BF16) for h in range(2)]
-        xq = {(a, h): tl("xq%d%d" % (a, h), [P, HALF], I32) for a in range(2) for h in range(2)}
-        xs = {(a, h): tl("xs%d%d" % (a, h), [P, HALF], U8) for a in range(2) for h in range(2)}
-        hq = [tl("hq%d" % h, [P, HALF], I32) for h in range(2)]
+        xq = {(a, h): tl("xq%d%d" % (a, h), [P, HALF], U32) for a in range(PASSES) for h in range(2)}
+        xs = {(a, h): tl("xs%d%d" % (a, h), [P, HALF], U8) for a in range(PASSES) for h in range(2)}
+        hq = [tl("hq%d" % h, [P, HALF], U32) for h in range(2)]
         hs = [tl("hs%d" % h, [P, HALF], U8) for h in range(2)]
-        x0_sb, xr_sb = {}, {}
         res = [tl("res%d" % c, [P, T], F32) for c in range(NT)]
         prod = [tl("prod%d" % c, [P, T], F32) for c in range(NT)]
-        xg, hg, hbank, ybank = {}, {}, {}, {}
+        x0_sb, xr_sb = {}, {}
+        hg = {(h, u): tl("hg%d%d" % (h, u), [P, 2 * CH * PACK], BF16) for h in range(2) for u in range(2)}
+        xg, hbank, ybank = {}, {}, {}
 
-        def load_scales(eng, plane, scales, quads, row0=0):
-            for q in quads:
-                eng.dma_start(
-                    out=plane[32 * q + row0 : 32 * q + row0 + 4].bitcast(I32),
-                    in_=scales[:, 4 * q : 4 * q + 4, :].rearrange("a r n -> r a n").bitcast(I32),
-                )
+        def load_scale_rows(plane, scales, r, row0):
+            nc.sync.dma_start(
+                out=plane[row0 + r : P : 32, 0 : scales.shape[0], :].bitcast(I32),
+                in_=scales[:, r::4, :].rearrange("a q n -> q a n").bitcast(I32),
+            )
 
-        def zero(eng, plane):
-            eng.memset(plane[:].rearrange("p a n -> p (a n)").bitcast(I32), 0)
+        def zero(plane):
+            nc.gpsimd.memset(plane[:].rearrange("p a n -> p (a n)").bitcast(I32), 0)
 
-        def cast(eng, a, h, c0, c1):
-            w = (c1 - c0) * CH
-            g = tl("xg%d%d%d" % (a, h, c0), [P, w * PACK], BF16)
-            xg[a, h, c0] = g
-            src = x_first[:, :, h * HALF + c0 * CH : h * HALF + c1 * CH]
-            o = g[:].rearrange("p (c i j) -> p c j i", i=4, j=PACK)
-            s = src.rearrange("p j (c i) -> p c j i", i=4)
+        def copy(eng, o, s):
             if eng == "v":
                 nc.vector.tensor_copy(out=o, in_=s)
             else:
                 nc.scalar.copy(out=o, in_=s)
+
+        def regroup_words(dst, src):
+            nc.vector.tensor_copy(
+                out=dst.bitcast(I32).rearrange("p (j mo mi) -> p mo j mi", j=PACK, mi=4),
+                in_=src.bitcast(I32).rearrange("p (mo mi j) -> p mo j mi", j=PACK, mi=4),
+            )
+
+        def regroup_scales(dst, src):
+            nc.vector.tensor_copy(
+                out=dst[:].rearrange("p a (j mo mi) -> p a mo j mi", j=PACK, mi=16),
+                in_=src[:].rearrange("p a (mo mi j) -> p a mo j mi", j=PACK, mi=16),
+            )
+
+        def regroup_wb(c0, c1):
+            nc.scalar.copy(
+                out=wb_w[:, c0:c1, :].rearrange("p c (am mi) -> p am c mi", mi=8),
+                in_=wb_raw[:].rearrange("p a (mo mi c) -> p (a mo) c mi", c=NT, mi=8)[:, :, c0:c1, :],
+            )
+
+        def regroup_wb_bytes(c):
+            nc.vector.tensor_copy(
+                out=wb_w[:, c, :].bitcast(U8).rearrange("p (m e) -> p m e", e=2),
+                in_=wb_raw[:].bitcast(U8).rearrange("p a (m c e) -> p (a m) c e", c=NT, e=2)[:, :, c, :],
+            )
+
+        def cast(eng, h, c0, c1):
+            g = tl("xg%d%d" % (h, c0), [P, (c1 - c0) * CH * PACK], BF16)
+            xg[h, c0] = g
+            src = x_first[:, :, h * HALF + c0 * CH : h * HALF + c1 * CH]
+            copy(eng, g[:].rearrange("p (c i j) -> p c j i", i=4, j=PACK), src.rearrange("p j (c i) -> p c j i", i=4))
 
         def cast_pair(eng, u, h, c0, c1):
             g = xg_last[h][:, c0 * CH * PACK : c1 * CH * PACK]
             o = g.rearrange("p (t j) -> p t j", j=PACK)[:, :, 2 * u : 2 * u + 2]
-            s = x_pair[u][:, :, h * HALF + c0 * CH : h * HALF + c1 * CH].rearrange("p j t -> p t j")
-            if eng == "v":
-                nc.vector.tensor_copy(out=o, in_=s)
-            else:
-                nc.scalar.copy(out=o, in_=s)
+            copy(eng, o, x_pair[u][:, :, h * HALF + c0 * CH : h * HALF + c1 * CH].rearrange("p j t -> p t j"))
 
         def quant_x(a, h, c0, c1):
             cols = slice(c0 * CH, c1 * CH)
-            g = xg[a, h, c0][:] if a == 0 else xg_last[h][:, c0 * CH * PACK : c1 * CH * PACK]
+            g = xg[h, c0][:] if a == 0 else xg_last[h][:, c0 * CH * PACK : c1 * CH * PACK]
             nc.vector.quantize_mx(out=xq[a, h][:, cols].bitcast(FP8X4), scales=xs[a, h][:, cols], in_=g)
 
         def h_mm(a, h, ch):
@@ -108,39 +132,32 @@ def tile_mix_cross_none_kernel(tc, x, wb_words, wb_scales, dn_words, dn_scales, 
                     stop=(a == PASSES - 1 and j == PACK - 1),
                 )
 
-        def h_copy(h, ch, eng="s"):
-            if ch % 2 == 0:
-                hg[h, ch // 2] = tl("hg%d%d" % (h, ch), [P, 2 * CH * PACK], BF16)
+        def h_copy(eng, h, ch):
             g = hg[h, ch // 2][:, (ch % 2) * CH * PACK : (ch % 2 + 1) * CH * PACK]
-            o = g.rearrange("p (t j) -> p t j", j=PACK)
-            s = hbank[h, ch][:].rearrange("p j t -> p t j")
-            if eng == "v":
-                nc.vector.tensor_copy(out=o, in_=s)
-            else:
-                nc.scalar.copy(out=o, in_=s)
+            copy(eng, g.rearrange("p (t j) -> p t j", j=PACK), hbank[h, ch][:].rearrange("p j t -> p t j"))
 
-        def quant_h(h, c0, c1):
-            cols = slice(c0 * CH, c1 * CH)
+        def quant_h(h, c0):
+            cols = slice(c0 * CH, (c0 + 2) * CH)
             nc.vector.quantize_mx(out=hq[h][:, cols].bitcast(FP8X4), scales=hs[h][:, cols], in_=hg[h, c0 // 2][:])
 
-        def y_wb(a, h, c):
-            if a == 0:
-                ybank[h, c] = ps.tile([P, HALF], F32, name="bank%d" % (2 * c + h))
-            nc.tensor.matmul_mx(
-                out=ybank[h, c][:],
-                lhsT=wb_w[:, a, 2 * c * P : 2 * (c + 1) * P].bitcast(FP4X4),
-                lhsT_scale=wb_s[:, a, c * P : (c + 1) * P],
-                rhs=xq[a, h][:].bitcast(FP8X4),
-                rhs_scale=xs[a, h][:],
-                start=(a == 0),
-                stop=False,
-            )
+        def y_wb(c, h):
+            ybank[c, h] = ps.tile([P, HALF], F32, name="bank%d" % (2 * c + h))
+            for a in range(PASSES):
+                nc.tensor.matmul_mx(
+                    out=ybank[c, h][:],
+                    lhsT=wb_w[:, c, a * P : (a + 1) * P].bitcast(U8).bitcast(FP4X4),
+                    lhsT_scale=y_s[:, a, c * P : (c + 1) * P],
+                    rhs=xq[a, h][:].bitcast(FP8X4),
+                    rhs_scale=xs[a, h][:],
+                    start=(a == 0),
+                    stop=False,
+                )
 
-        def y_up(h, c):
+        def y_up(c, h):
             nc.tensor.matmul_mx(
-                out=ybank[h, c][:],
+                out=ybank[c, h][:],
                 lhsT=up_w[:, c * P : (c + 1) * P].bitcast(FP8X4),
-                lhsT_scale=up_s[UP_ROW:P, 0, c * P : (c + 1) * P],
+                lhsT_scale=y_s[UP_ROW:P, 0, c * P : (c + 1) * P],
                 rhs=hq[h][:].bitcast(FP8X4),
                 rhs_scale=hs[h][:],
                 start=False,
@@ -149,92 +166,62 @@ def tile_mix_cross_none_kernel(tc, x, wb_words, wb_scales, dn_words, dn_scales, 
 
         def gate(c, h):
             cols = slice(h * HALF, (h + 1) * HALF)
-            nc.vector.scalar_tensor_tensor(out=prod[c][:, cols], in0=ybank[h, c][:], scalar=b_t[:, 32 * c : 32 * c + 1], in1=x0_sb[c][:, cols], op0=ADD, op1=MULT)
+            nc.vector.scalar_tensor_tensor(out=prod[c][:, cols], in0=ybank[c, h][:], scalar=b_sb[:, c : c + 1], in1=x0_sb[c][:, cols], op0=ADD, op1=MULT)
 
-        def resid(e, c, t0, t1):
-            e.tensor_tensor(out=res[c][:, t0:t1], in0=prod[c][:, t0:t1], in1=xr_sb[c][:, t0:t1], op=ADD)
-
-        def yw(h, c):
-            y_wb(0, h, c)
-            y_wb(1, h, c)
-
-        def perm_words(a):
-            nc.vector.tensor_copy(
-                out=dn_w[a][:].rearrange("p (j mo mi) -> p mo j mi", j=PACK, mi=4),
-                in_=dn_raw[:, a, :].rearrange("p (mo mi j) -> p mo j mi", j=PACK, mi=4),
-            )
-
-        def perm_s(a):
-            nc.vector.tensor_copy(
-                out=dn_s[:, a, :].rearrange("p (j mo mi) -> p mo j mi", j=PACK, mi=16),
-                in_=dn_sraw[:, a, :].rearrange("p (mo mi j) -> p mo j mi", j=PACK, mi=16),
-            )
-
-        def bias():
-            nc.vector.transpose(b_t[:], b_rows[:])
-
-        def prep_x(a, h, on_vector):
-            for ch in range(on_vector):
-                cast("v", a, h, ch, ch + 1)
-            for ch in range(on_vector, NCH):
-                cast("s", a, h, ch, ch + 1)
-            for ch in range(NCH):
-                quant_x(a, h, ch, ch + 1)
+        def resid(eng, c, t0, t1):
+            eng.tensor_tensor(out=res[c][:, t0:t1], in0=prod[c][:, t0:t1], in1=xr_sb[c][:, t0:t1], op=ADD)
 
         xv = x.rearrange("(a p j) t -> a p j t", p=P, j=PACK)
 
+        def by_tile(src):
+            return src.rearrange("(p c) t -> p c t", c=NT)
+
         def load_rows(name, dst, src, c0, c1):
             t = tl("%s_rows%d" % (name, c0), [P, c1 - c0, T], F32)
-            nc.sync.dma_start(out=t[:], in_=src[c0 * P : c1 * P, :].rearrange("(c p) t -> p c t", p=P))
+            nc.sync.dma_start(out=t[:], in_=by_tile(src)[:, c0:c1, :])
             for c in range(c0, c1):
                 dst[c] = t[:, c - c0, :]
 
         def store(c, t0=0, t1=T):
-            nc.sync.dma_start(out=out[c * P : (c + 1) * P, t0:t1], in_=res[c][:, t0:t1])
+            nc.sync.dma_start(out=by_tile(out)[:, c, t0:t1], in_=res[c][:, t0:t1])
 
-        zero(nc.gpsimd, dn_sraw)
-        nc.gpsimd.memset(b_rows[:], 0.0)
-        zero(nc.vector, wb_s)
-        zero(nc.vector, up_s)
+        zero(dn_sraw)
+        zero(y_sraw)
 
-        nc.sync.dma_start(out=dn_raw[:], in_=dn_words.rearrange("a p r i -> p a (r i)").bitcast(I32))
-        load_scales(nc.sync, dn_sraw, dn_scales, range(4), DN_ROW)
-        nc.sync.dma_start(out=b_rows[0:P:32, :].rearrange("q (c i) -> q c i", i=32), in_=b.rearrange("(c q i) -> q c i", q=4, i=32))
+        nc.sync.dma_start(out=dn_raw[:].bitcast(I32), in_=dn_words.rearrange("a p r i -> p a (r i)").bitcast(I32))
+        for r in range(4):
+            load_scale_rows(dn_sraw, dn_scales, r, DN_ROW)
         nc.sync.dma_start(out=x_first[:], in_=xv[0])
-        load_scales(nc.sync, wb_s, wb_scales, range(3))
-        nc.sync.dma_start(out=x_pair[0][:], in_=xv[1][:, 0:2, :])
-        load_scales(nc.sync, wb_s, wb_scales, [3])
-        load_scales(nc.sync, up_s, upw_scales, [0], UP_ROW)
-        nc.sync.dma_start(out=x_pair[1][:], in_=xv[1][:, 2:4, :])
-        nc.sync.dma_start(out=wb_w[:].bitcast(I32), in_=wb_words.rearrange("a p n -> p a n").bitcast(I32))
-        nc.sync.dma_start(out=up_w[:], in_=upw_words[0].rearrange("p n i -> p (n i)").bitcast(I32))
+        for u in range(2):
+            for r in range(2 * u, 2 * u + 2):
+                load_scale_rows(y_sraw, wb_scales, r, WB_ROW)
+                load_scale_rows(y_sraw, upw_scales, r, UP_ROW)
+            nc.sync.dma_start(out=x_pair[u][:], in_=xv[1][:, 2 * u : 2 * u + 2, :])
+        nc.sync.dma_start(out=wb_raw[:].bitcast(I32), in_=wb_words.rearrange("a p n -> p a n").bitcast(I32))
+        nc.sync.dma_start(out=up_raw[:].bitcast(I32), in_=upw_words[0].rearrange("p n i -> p (n i)").bitcast(I32))
+        nc.sync.dma_start(out=b_sb[:], in_=b.rearrange("(p c) -> p c", c=NT))
         load_rows("x0", x0_sb, x0, 0, 2)
-        load_scales(nc.sync, up_s, upw_scales, range(1, 4), UP_ROW)
-        load_rows("xr", xr_sb, xr, 0, 1)
-        load_rows("xr", xr_sb, xr, 1, 2)
-        for c in range(2, NT):
-            load_rows("x0", x0_sb, x0, c, c + 1)
-            load_rows("xr", xr_sb, xr, c, c + 1)
+        load_rows("xr", xr_sb, xr, 0, 2)
+        load_rows("x0", x0_sb, x0, 2, 4)
+        load_rows("xr", xr_sb, xr, 2, 3)
+        load_rows("xr", xr_sb, xr, 3, 4)
 
         for a in range(PASSES):
-            perm_words(a)
-        for a in range(PASSES):
-            perm_s(a)
-        bias()
+            regroup_words(dn_w[a][:], dn_raw[:, a, :])
+        regroup_scales(dn_s, dn_sraw)
 
-        cast("v", 0, 0, 0, 1)
-        cast("s", 0, 0, 2, 4)
-        cast("v", 0, 0, 1, 2)
-        quant_x(0, 0, 0, 1)
-        cast("s", 0, 1, 2, 4)
-        quant_x(0, 0, 1, 2)
-        cast("v", 0, 1, 0, 2)
+        cast("v", 0, 0, 2)
+        cast("s", 0, 2, 4)
+        cast("s", 1, 2, 4)
+        cast("v", 1, 0, 2)
+        quant_x(0, 0, 0, 2)
         quant_x(0, 0, 2, 4)
+        cast_pair("s", 0, 1, 2, 4)
         quant_x(0, 1, 0, 2)
         cast_pair("v", 0, 0, 0, 4)
-        cast_pair("s", 0, 1, 2, 4)
-        quant_x(0, 1, 2, 4)
         cast_pair("v", 0, 1, 0, 2)
+        quant_x(0, 1, 2, 4)
+        regroup_scales(y_s, y_sraw)
         for h in range(2):
             for ch in range(NCH):
                 h_mm(0, h, ch)
@@ -254,50 +241,53 @@ def tile_mix_cross_none_kernel(tc, x, wb_words, wb_scales, dn_words, dn_scales, 
         for h in range(2):
             for ch in range(NCH):
                 h_mm(1, h, ch)
-        h_copy(0, 0)
-        h_copy(0, 1)
-        h_copy(0, 2)
-        h_copy(0, 3, "v")
-        quant_h(0, 0, 2)
-        h_copy(1, 0)
-        h_copy(1, 1)
-        h_copy(1, 2)
-        quant_h(0, 2, 4)
-        h_copy(1, 3, "v")
-        yw(0, 0)
+        h_copy("s", 0, 0)
+        regroup_words(up_w[:], up_raw[:])
+        h_copy("s", 0, 1)
+        h_copy("s", 0, 2)
+        regroup_wb(0, 1)
+        h_copy("v", 0, 3)
+        quant_h(0, 0)
+        quant_h(0, 2)
+        h_copy("v", 1, 3)
+        for ch in range(NCH - 1):
+            h_copy("s", 1, ch)
+        regroup_wb_bytes(1)
+        regroup_wb(2, 4)
+        y_wb(0, 0)
         y_up(0, 0)
-        yw(1, 0)
-        quant_h(1, 0, 2)
-        quant_h(1, 2, 4)
-        yw(0, 1)
-        y_up(1, 0)
+        y_wb(0, 1)
+        y_wb(1, 0)
+        quant_h(1, 0)
+        quant_h(1, 2)
         y_up(0, 1)
-        yw(1, 1)
+        y_up(1, 0)
+        y_wb(1, 1)
         y_up(1, 1)
         for c in range(2, NT):
             for h in range(2):
-                yw(h, c)
-                y_up(h, c)
+                y_wb(c, h)
+                y_up(c, h)
         gate(0, 0)
-        resid(nc.gpsimd, 0, 0, 512)
+        resid(nc.gpsimd, 0, 0, 448)
         gate(0, 1)
         gate(1, 0)
-        resid(nc.vector, 0, 512, T)
+        resid(nc.vector, 0, 448, T)
         store(0)
         resid(nc.gpsimd, 1, 0, 448)
         gate(1, 1)
         gate(2, 0)
         resid(nc.vector, 1, 448, T)
         store(1)
-        resid(nc.gpsimd, 2, 0, HALF)
-        store(2, 0, HALF)
+        resid(nc.gpsimd, 2, 0, 448)
+        store(2, 0, 448)
         gate(2, 1)
         gate(3, 0)
-        resid(nc.vector, 2, HALF, T)
-        store(2, HALF, T)
-        resid(nc.gpsimd, 3, 0, 256)
+        resid(nc.vector, 2, 448, T)
+        store(2, 448, T)
+        resid(nc.gpsimd, 3, 0, 192)
         gate(3, 1)
-        resid(nc.vector, 3, 256, HALF)
+        resid(nc.vector, 3, 192, HALF)
         store(3, 0, HALF)
         resid(nc.vector, 3, HALF, T)
         store(3, HALF, T)

@@ -101,6 +101,14 @@ def tile_mix_cross_none_kernel(tc, x, wb_words, wb_scales, dn_words, dn_scales, 
                 in_=wb_raw[:].bitcast(U8).rearrange("p a (m c e) -> p (a m) c e", c=NT, e=2)[:, :, c, :],
             )
 
+        def regroup_up(eng, c0, c1):
+            view = I32 if eng == "v" else U32
+            copy(
+                eng,
+                up_w[:, c0 * P : c1 * P].bitcast(view).rearrange("p (c m) -> p m c", c=c1 - c0),
+                up_raw[:].bitcast(view).rearrange("p (m c) -> p m c", c=NT)[:, :, c0:c1],
+            )
+
         def cast(eng, h, c0, c1):
             g = tl("xg%d%d" % (h, c0), [P, (c1 - c0) * CH * PACK], BF16)
             xg[h, c0] = g
@@ -201,23 +209,26 @@ def tile_mix_cross_none_kernel(tc, x, wb_words, wb_scales, dn_words, dn_scales, 
         nc.sync.dma_start(out=up_raw[:].bitcast(I32), in_=upw_words[0].rearrange("p n i -> p (n i)").bitcast(I32))
         nc.sync.dma_start(out=b_sb[:], in_=b.rearrange("(p c) -> p c", c=NT))
         load_rows("x0", x0_sb, x0, 0, 2)
-        load_rows("xr", xr_sb, xr, 0, 2)
-        load_rows("x0", x0_sb, x0, 2, 4)
-        load_rows("xr", xr_sb, xr, 2, 3)
-        load_rows("xr", xr_sb, xr, 3, 4)
+        load_rows("xr", xr_sb, xr, 0, 1)
+        load_rows("xr", xr_sb, xr, 1, 2)
+        for c in range(2, NT):
+            load_rows("x0", x0_sb, x0, c, c + 1)
+            load_rows("xr", xr_sb, xr, c, c + 1)
 
         for a in range(PASSES):
             regroup_words(dn_w[a][:], dn_raw[:, a, :])
         regroup_scales(dn_s, dn_sraw)
 
-        cast("v", 0, 0, 2)
+        cast("v", 0, 0, 1)
         cast("s", 0, 2, 4)
         cast("s", 1, 2, 4)
+        cast("v", 0, 1, 2)
+        quant_x(0, 0, 0, 1)
+        quant_x(0, 0, 1, 2)
         cast("v", 1, 0, 2)
-        quant_x(0, 0, 0, 2)
         quant_x(0, 0, 2, 4)
-        cast_pair("s", 0, 1, 2, 4)
         quant_x(0, 1, 0, 2)
+        cast_pair("s", 0, 1, 2, 4)
         cast_pair("v", 0, 0, 0, 4)
         cast_pair("v", 0, 1, 0, 2)
         quant_x(0, 1, 2, 4)
@@ -242,7 +253,7 @@ def tile_mix_cross_none_kernel(tc, x, wb_words, wb_scales, dn_words, dn_scales, 
             for ch in range(NCH):
                 h_mm(1, h, ch)
         h_copy("s", 0, 0)
-        regroup_words(up_w[:], up_raw[:])
+        regroup_up("v", 0, 2)
         h_copy("s", 0, 1)
         h_copy("s", 0, 2)
         regroup_wb(0, 1)
@@ -254,6 +265,7 @@ def tile_mix_cross_none_kernel(tc, x, wb_words, wb_scales, dn_words, dn_scales, 
             h_copy("s", 1, ch)
         regroup_wb_bytes(1)
         regroup_wb(2, 4)
+        regroup_up("s", 2, 4)
         y_wb(0, 0)
         y_up(0, 0)
         y_wb(0, 1)
@@ -269,25 +281,25 @@ def tile_mix_cross_none_kernel(tc, x, wb_words, wb_scales, dn_words, dn_scales, 
                 y_wb(c, h)
                 y_up(c, h)
         gate(0, 0)
-        resid(nc.gpsimd, 0, 0, 448)
+        resid(nc.gpsimd, 0, 0, 512)
         gate(0, 1)
         gate(1, 0)
-        resid(nc.vector, 0, 448, T)
+        resid(nc.vector, 0, 512, T)
         store(0)
         resid(nc.gpsimd, 1, 0, 448)
         gate(1, 1)
         gate(2, 0)
         resid(nc.vector, 1, 448, T)
         store(1)
-        resid(nc.gpsimd, 2, 0, 448)
-        store(2, 0, 448)
+        resid(nc.gpsimd, 2, 0, 512)
+        store(2, 0, 512)
         gate(2, 1)
         gate(3, 0)
-        resid(nc.vector, 2, 448, T)
-        store(2, 448, T)
-        resid(nc.gpsimd, 3, 0, 192)
+        resid(nc.vector, 2, 512, T)
+        store(2, 512, T)
+        resid(nc.gpsimd, 3, 0, 256)
         gate(3, 1)
-        resid(nc.vector, 3, 192, HALF)
-        store(3, 0, HALF)
-        resid(nc.vector, 3, HALF, T)
-        store(3, HALF, T)
+        resid(nc.vector, 3, 256, 512)
+        store(3, 0, 512)
+        resid(nc.vector, 3, 512, T)
+        store(3, 512, T)

from contextlib import ExitStack

import concourse.mybir as mybir

K, R, N, T = 1024, 512, 512, 1024
FLOPS = 2 * T * (K * R + K * N + R * N)

F32 = mybir.dt.float32
BF16 = mybir.dt.bfloat16
I32 = mybir.dt.int32
U32 = mybir.dt.uint32
U16 = mybir.dt.uint16
U8 = mybir.dt.uint8
FP8X4 = mybir.dt.float8_e4m3fn_x4
FP4X4 = mybir.dt.float4_e2m1fn_x4
ADD = mybir.AluOpType.add
MULT = mybir.AluOpType.mult

P = 128
PACK = 4
PASSES = K // (P * PACK)
HALF = 512
CH = 128
NCH = HALF // CH
NT = N // P
WB_ROW = 0
DN_ROW = 4
UP_ROW = 8


def tile_mix_cross_none_kernel(tc, x, wb_words, wb_scales, dn_words, dn_scales, upw_words, upw_scales, x0, b, xr, out):
    nc = tc.nc
    with ExitStack() as ctx:
        sb = ctx.enter_context(tc.tile_pool(name="sb", bufs=1))
        ps = ctx.enter_context(tc.psum_pool(name="ps", bufs=1))
        ctx.enter_context(tc.manual_schedule())

        def tl(name, shape, dtype):
            return sb.tile(shape, dtype, name=name, align_bytes=64)

        dn_raw = tl("dn_raw", [P, PASSES, R], U32)
        dn_w = [tl("dn_w%d" % a, [P, R], U32) for a in range(PASSES)]
        dn_sraw = tl("dn_sraw", [P, PASSES, R], U8)
        dn_s = tl("dn_s", [P, PASSES, R], U8)
        wb_raw = tl("wb_raw", [P, PASSES, N], U16)
        wb_w = tl("wb_w", [P, NT, PASSES * P], U16)
        up_raw = tl("up_raw", [P, N], U32)
        up_w = tl("up_w", [P, N], U32)
        y_sraw = tl("y_sraw", [P, PASSES, N], U8)
        y_s = tl("y_s", [P, PASSES, N], U8)
        b_sb = tl("b_sb", [P, NT], F32)
        x_first = tl("x_first", [P, PACK, T], F32)
        x_pair = [tl("x_pair%d" % u, [P, 2, T], F32) for u in range(2)]
        xg_last = [tl("xg_last%d" % h, [P, HALF * PACK], BF16) for h in range(2)]
        xq = {(a, h): tl("xq%d%d" % (a, h), [P, HALF], U32) for a in range(PASSES) for h in range(2)}
        xs = {(a, h): tl("xs%d%d" % (a, h), [P, HALF], U8) for a in range(PASSES) for h in range(2)}
        hq = [tl("hq%d" % h, [P, HALF], U32) for h in range(2)]
        hs = [tl("hs%d" % h, [P, HALF], U8) for h in range(2)]
        res = [tl("res%d" % c, [P, T], F32) for c in range(NT)]
        prod = [tl("prod%d" % c, [P, T], F32) for c in range(NT)]
        x0_sb, xr_sb = {}, {}
        hg = {(h, u): tl("hg%d%d" % (h, u), [P, 2 * CH * PACK], BF16) for h in range(2) for u in range(2)}
        xg, hbank, ybank = {}, {}, {}

        def load_scale_rows(plane, scales, r, row0):
            nc.sync.dma_start(
                out=plane[row0 + r : P : 32, 0 : scales.shape[0], :].bitcast(I32),
                in_=scales[:, r::4, :].rearrange("a q n -> q a n").bitcast(I32),
            )

        def zero(plane):
            nc.gpsimd.memset(plane[:].rearrange("p a n -> p (a n)").bitcast(I32), 0)

        def copy(eng, o, s):
            if eng == "v":
                nc.vector.tensor_copy(out=o, in_=s)
            else:
                nc.scalar.copy(out=o, in_=s)

        def regroup_words(dst, src):
            nc.vector.tensor_copy(
                out=dst.bitcast(I32).rearrange("p (j mo mi) -> p mo j mi", j=PACK, mi=4),
                in_=src.bitcast(I32).rearrange("p (mo mi j) -> p mo j mi", j=PACK, mi=4),
            )

        def regroup_scales(dst, src):
            nc.vector.tensor_copy(
                out=dst[:].rearrange("p a (j mo mi) -> p a mo j mi", j=PACK, mi=16),
                in_=src[:].rearrange("p a (mo mi j) -> p a mo j mi", j=PACK, mi=16),
            )

        def regroup_wb(c0, c1):
            nc.scalar.copy(
                out=wb_w[:, c0:c1, :].rearrange("p c (am mi) -> p am c mi", mi=8),
                in_=wb_raw[:].rearrange("p a (mo mi c) -> p (a mo) c mi", c=NT, mi=8)[:, :, c0:c1, :],
            )

        def regroup_wb_bytes(c):
            nc.vector.tensor_copy(
                out=wb_w[:, c, :].bitcast(U8).rearrange("p (m e) -> p m e", e=2),
                in_=wb_raw[:].bitcast(U8).rearrange("p a (m c e) -> p (a m) c e", c=NT, e=2)[:, :, c, :],
            )

        def regroup_up(eng, c0, c1):
            view = I32 if eng == "v" else U32
            copy(
                eng,
                up_w[:, c0 * P : c1 * P].bitcast(view).rearrange("p (c m) -> p m c", c=c1 - c0),
                up_raw[:].bitcast(view).rearrange("p (m c) -> p m c", c=NT)[:, :, c0:c1],
            )

        def cast(eng, h, c0, c1):
            g = tl("xg%d%d" % (h, c0), [P, (c1 - c0) * CH * PACK], BF16)
            xg[h, c0] = g
            src = x_first[:, :, h * HALF + c0 * CH : h * HALF + c1 * CH]
            copy(eng, g[:].rearrange("p (c i j) -> p c j i", i=4, j=PACK), src.rearrange("p j (c i) -> p c j i", i=4))

        def cast_pair(eng, u, h, c0, c1):
            g = xg_last[h][:, c0 * CH * PACK : c1 * CH * PACK]
            o = g.rearrange("p (t j) -> p t j", j=PACK)[:, :, 2 * u : 2 * u + 2]
            copy(eng, o, x_pair[u][:, :, h * HALF + c0 * CH : h * HALF + c1 * CH].rearrange("p j t -> p t j"))

        def quant_x(a, h, c0, c1):
            cols = slice(c0 * CH, c1 * CH)
            g = xg[h, c0][:] if a == 0 else xg_last[h][:, c0 * CH * PACK : c1 * CH * PACK]
            nc.vector.quantize_mx(out=xq[a, h][:, cols].bitcast(FP8X4), scales=xs[a, h][:, cols], in_=g)

        def h_mm(a, h, ch):
            if a == 0:
                hbank[h, ch] = ps.tile([P, PACK, CH], F32, name="bank%d" % (NCH * h + ch))
            cols = slice(ch * CH, (ch + 1) * CH)
            for j in range(PACK):
                nc.tensor.matmul_mx(
                    out=hbank[h, ch][:, j, :],
                    lhsT=dn_w[a][:, j * P : (j + 1) * P].bitcast(FP8X4),
                    lhsT_scale=dn_s[DN_ROW:P, a, j * P : (j + 1) * P],
                    rhs=xq[a, h][:, cols].bitcast(FP8X4),
                    rhs_scale=xs[a, h][:, cols],
                    start=(a == 0 and j == 0),
                    stop=(a == PASSES - 1 and j == PACK - 1),
                )

        def h_copy(eng, h, ch):
            g = hg[h, ch // 2][:, (ch % 2) * CH * PACK : (ch % 2 + 1) * CH * PACK]
            copy(eng, g.rearrange("p (t j) -> p t j", j=PACK), hbank[h, ch][:].rearrange("p j t -> p t j"))

        def quant_h(h, c0):
            cols = slice(c0 * CH, (c0 + 2) * CH)
            nc.vector.quantize_mx(out=hq[h][:, cols].bitcast(FP8X4), scales=hs[h][:, cols], in_=hg[h, c0 // 2][:])

        def y_wb(c, h):
            ybank[c, h] = ps.tile([P, HALF], F32, name="bank%d" % (2 * c + h))
            for a in range(PASSES):
                nc.tensor.matmul_mx(
                    out=ybank[c, h][:],
                    lhsT=wb_w[:, c, a * P : (a + 1) * P].bitcast(U8).bitcast(FP4X4),
                    lhsT_scale=y_s[:, a, c * P : (c + 1) * P],
                    rhs=xq[a, h][:].bitcast(FP8X4),
                    rhs_scale=xs[a, h][:],
                    start=(a == 0),
                    stop=False,
                )

        def y_up(c, h):
            nc.tensor.matmul_mx(
                out=ybank[c, h][:],
                lhsT=up_w[:, c * P : (c + 1) * P].bitcast(FP8X4),
                lhsT_scale=y_s[UP_ROW:P, 0, c * P : (c + 1) * P],
                rhs=hq[h][:].bitcast(FP8X4),
                rhs_scale=hs[h][:],
                start=False,
                stop=True,
            )

        def gate(c, h):
            cols = slice(h * HALF, (h + 1) * HALF)
            nc.vector.scalar_tensor_tensor(out=prod[c][:, cols], in0=ybank[c, h][:], scalar=b_sb[:, c : c + 1], in1=x0_sb[c][:, cols], op0=ADD, op1=MULT)

        def resid(eng, c, t0, t1):
            eng.tensor_tensor(out=res[c][:, t0:t1], in0=prod[c][:, t0:t1], in1=xr_sb[c][:, t0:t1], op=ADD)

        xv = x.rearrange("(a p j) t -> a p j t", p=P, j=PACK)

        def by_tile(src):
            return src.rearrange("(p c) t -> p c t", c=NT)

        def load_rows(name, dst, src, c0, c1):
            t = tl("%s_rows%d" % (name, c0), [P, c1 - c0, T], F32)
            nc.sync.dma_start(out=t[:], in_=by_tile(src)[:, c0:c1, :])
            for c in range(c0, c1):
                dst[c] = t[:, c - c0, :]

        def store(c, t0=0, t1=T):
            nc.sync.dma_start(out=by_tile(out)[:, c, t0:t1], in_=res[c][:, t0:t1])

        zero(dn_sraw)
        zero(y_sraw)

        nc.sync.dma_start(out=dn_raw[:].bitcast(I32), in_=dn_words.rearrange("a p r i -> p a (r i)").bitcast(I32))
        for r in range(4):
            load_scale_rows(dn_sraw, dn_scales, r, DN_ROW)
        nc.sync.dma_start(out=x_first[:], in_=xv[0])
        for u in range(2):
            for r in range(2 * u, 2 * u + 2):
                load_scale_rows(y_sraw, wb_scales, r, WB_ROW)
                load_scale_rows(y_sraw, upw_scales, r, UP_ROW)
            nc.sync.dma_start(out=x_pair[u][:], in_=xv[1][:, 2 * u : 2 * u + 2, :])
        nc.sync.dma_start(out=wb_raw[:].bitcast(I32), in_=wb_words.rearrange("a p n -> p a n").bitcast(I32))
        nc.sync.dma_start(out=up_raw[:].bitcast(I32), in_=upw_words[0].rearrange("p n i -> p (n i)").bitcast(I32))
        nc.sync.dma_start(out=b_sb[:], in_=b.rearrange("(p c) -> p c", c=NT))
        load_rows("x0", x0_sb, x0, 0, 2)
        load_rows("xr", xr_sb, xr, 0, 1)
        load_rows("xr", xr_sb, xr, 1, 2)
        for c in range(2, NT):
            load_rows("x0", x0_sb, x0, c, c + 1)
            load_rows("xr", xr_sb, xr, c, c + 1)

        for a in range(PASSES):
            regroup_words(dn_w[a][:], dn_raw[:, a, :])
        regroup_scales(dn_s, dn_sraw)

        cast("v", 0, 0, 1)
        cast("s", 0, 2, 4)
        cast("s", 1, 2, 4)
        cast("v", 0, 1, 2)
        quant_x(0, 0, 0, 1)
        quant_x(0, 0, 1, 2)
        cast("v", 1, 0, 2)
        quant_x(0, 0, 2, 4)
        quant_x(0, 1, 0, 2)
        cast_pair("s", 0, 1, 2, 4)
        cast_pair("v", 0, 0, 0, 4)
        cast_pair("v", 0, 1, 0, 2)
        quant_x(0, 1, 2, 4)
        regroup_scales(y_s, y_sraw)
        for h in range(2):
            for ch in range(NCH):
                h_mm(0, h, ch)

        cast_pair("v", 1, 0, 0, 1)
        cast_pair("s", 1, 0, 2, 3)
        cast_pair("v", 1, 0, 1, 2)
        cast_pair("s", 1, 1, 0, 1)
        cast_pair("s", 1, 1, 1, 2)
        quant_x(1, 0, 0, 1)
        cast_pair("v", 1, 0, 3, 4)
        quant_x(1, 0, 1, 3)
        cast_pair("v", 1, 1, 2, 4)
        quant_x(1, 0, 3, 4)
        quant_x(1, 1, 0, 2)
        quant_x(1, 1, 2, 4)
        for h in range(2):
            for ch in range(NCH):
                h_mm(1, h, ch)
        h_copy("s", 0, 0)
        regroup_up("v", 0, 2)
        h_copy("s", 0, 1)
        h_copy("s", 0, 2)
        regroup_wb(0, 1)
        h_copy("v", 0, 3)
        quant_h(0, 0)
        quant_h(0, 2)
        h_copy("v", 1, 3)
        for ch in range(NCH - 1):
            h_copy("s", 1, ch)
        regroup_wb_bytes(1)
        regroup_wb(2, 4)
        regroup_up("s", 2, 4)
        y_wb(0, 0)
        y_up(0, 0)
        y_wb(0, 1)
        y_wb(1, 0)
        quant_h(1, 0)
        quant_h(1, 2)
        y_up(0, 1)
        y_up(1, 0)
        y_wb(1, 1)
        y_up(1, 1)
        for c in range(2, NT):
            for h in range(2):
                y_wb(c, h)
                y_up(c, h)
        gate(0, 0)
        resid(nc.gpsimd, 0, 0, 512)
        gate(0, 1)
        gate(1, 0)
        resid(nc.vector, 0, 512, T)
        store(0)
        resid(nc.gpsimd, 1, 0, 448)
        gate(1, 1)
        gate(2, 0)
        resid(nc.vector, 1, 448, T)
        store(1)
        resid(nc.gpsimd, 2, 0, 512)
        store(2, 0, 512)
        gate(2, 1)
        gate(3, 0)
        resid(nc.vector, 2, 512, T)
        store(2, 512, T)
        resid(nc.gpsimd, 3, 0, 256)
        gate(3, 1)
        resid(nc.vector, 3, 256, 512)
        store(3, 0, 512)
        resid(nc.vector, 3, 512, T)
        store(3, 512, T)
